import numpy as np, ml_dtypes
CORES = [40,64,80,88,96,104,120,144]
N = 8
import mx_ref
BF = ml_dtypes.bfloat16
def pick(q, e):
    c = np.concatenate([q[0].reshape(128, -1, 4), np.zeros((128, 1, 4), np.uint8)], axis=1); s = np.concatenate([q[1], np.ones((16, 1), np.uint8)], axis=1)
    return (np.ascontiguousarray(c[:, e].reshape(128, -1)), np.ascontiguousarray(s[:, e]))
def join(*qs):
    return (np.concatenate([q[0] for q in qs], axis=1), np.concatenate([q[1] for q in qs], axis=1))
def put(q, e, v):
    c, s = q[0].reshape(128, -1, 4).copy(), q[1].copy(); c[:, e] = v[0].reshape(128, -1, 4); s[:, e] = v[1]
    return (c.reshape(128, -1), s)
def pk(c, s):
    return (np.ascontiguousarray(c), mx_ref.live(s))
def emit(q):
    return q[0], q[1]
def decode(q):
    o = []
    for b in range(4):
        e = np.zeros((128, 128, 4), np.float32); e[np.arange(128), np.arange(128), b] = 1
        o.append(mx_ref.matmul(mx_ref.quantize(e.reshape(128, 512).astype(BF)), q))
    return np.stack(o, axis=2).reshape(128, -1)
def cols(t, e):
    v = np.concatenate([t.reshape(128, -1, 4), np.zeros((128, 1, 4), BF)], axis=1)
    return np.ascontiguousarray(v[:, e]).reshape(128, -1)
def cut(t, i, w=512):
    return t[:, w * i:w * i + w]
def f(rng, *shape):
    return mx_ref.flush((rng.standard_normal(shape, dtype=np.float32) * np.exp2(rng.integers(-2, 3, shape[:-1] + (1,)))).astype(BF))
def wide(rng, *shape, cols=0):
    v = rng.standard_normal(shape, dtype=np.float32) * np.exp2(rng.integers(-12, 13, shape)).astype(np.float32)
    if cols: v *= np.repeat(np.exp2(rng.integers(-cols, cols + 1, shape[:-2] + (1, shape[-1] // 4))) * (rng.random(shape[:-2] + (1, shape[-1] // 4)) > 0.0625), 4, axis=-1).astype(np.float32)
    return mx_ref.flush(v.astype(BF))
C, T, R, O = 128, 32, 3, 1
def trim(v):
    v = v.astype(np.float32)
    v[np.abs(v) < np.float32(2.0 ** -14)] = 0
    return v.astype(BF)
def given(rng, u, x):
    return {"kb": np.stack([trim(u.reshape(128, 4 * C))] * N), "x": trim(x.reshape(N, 128, 4 * R * T)), "w": f(rng, N, 128, 512 * O)}
def sturdy(rng, n):
    return (1 + rng.random((128, n, 4))) * rng.choice([-1.0, 1.0], (128, n, 4)) * np.exp2(rng.integers(-1, 2, (128, 1, 1)))
def kept(v):
    m, e = np.frexp(v)
    return np.ldexp(np.trunc(m * 8) * 0.125, e)
def near(rng, u, e):
    return u[:, e] + 0.5 * sturdy(rng, len(e))
def setup_inputs(rng):
    return given(rng, f(rng, 128, 4 * C), f(rng, N, 128, 4 * R * T))
def setup_inputs_both(rng):
    u, x, new = kept(sturdy(rng, C)), np.zeros((N, 128, R, T, 4)), np.zeros((N, C), bool)
    for b in range(R):
        for j, r in enumerate(rng.permutation([v for v in range(N) if v < v ^ (1 << b)])):
            p, e = r ^ (1 << b), rng.permutation(C)
            if j % 2: e = e[np.argsort(new[r, e] | ~new[p, e], kind="stable")]
            t = e[T:2 * T] if j % 2 else rng.permutation(e[:T])
            x[r, :, b] = near(rng, u, e[:T])
            x[r, :, b, :T // 4] = u[:, e[:T // 4]]
            x[p, :, b] = near(rng, u, t)
            for s in (r, p):
                new[s, e[:T]] = True
                new[s, t] = True
    return given(rng, u, x)
def setup_inputs_few(rng):
    u, x, four = sturdy(rng, C), np.zeros((N, 128, R, T, 4)), rng.permutation(C)[:4]
    for b in range(R):
        for j, r in enumerate(rng.permutation([v for v in range(N) if v < v ^ (1 << b)])):
            a = rng.permutation(four)[:2]
            for s, c in ((r, a[0]), (r ^ (1 << b), a[j % 2])):
                x[s, :, b] = near(rng, u, np.full(T, c)) * np.exp2(rng.integers(-1, 2, (1, T, 1)))
    return given(rng, u, x)
def setup_inputs_ties(rng):
    u = np.abs(cols(f(rng, 128, 4 * (C // 4)), rng.permutation(np.arange(C) % (C // 4))).astype(np.float32))
    x = np.abs(f(rng, N, 128, 4 * R * T).astype(np.float32)).reshape(N, 128, R, T, 4)
    for r in range(N):
        for b in range(R):
            x[r, :, b] *= (1 - 2 * (rng.permutation(T) % 2)).astype(np.float32)[:, None]
            x[r, :, b, int(rng.integers(0, T))] = 0
    return given(rng, u * np.float32(2.0 ** 18), x * np.float32(2.0 ** 18))
def setup_inputs_drift(rng):
    top = (rng.permutation(128) < 64)[:, None, None]
    u, z, x = sturdy(rng, C) * top, sturdy(rng, 8) * ~top, np.zeros((N, 128, R, T, 4))
    e = rng.permutation(C)
    for r in range(N):
        for b in range(R):
            t = rng.permutation(e[:C // 2] if b == 0 else e[C // 2:])[:T]
            x[r, :, b] = near(rng, u, t) * top + 8 * z[:, rng.permutation(np.arange(T) % 8)]
    return given(rng, u, x)
def setup_inputs_spread(rng):
    d = given(rng, wide(rng, 128, 4 * C, cols=2), wide(rng, N, 128, 4 * R * T, cols=6))
    d["kb"][:, :, :4] = BF(-0.0)
    for r in range(N):
        for b in range(R):
            i = 4 * (b * T + int(rng.integers(0, T)))
            d["x"][r, :, i:i + 4] = BF(0.0)
    return d
def check_inputs(d):
    b = []
    for n, lo, hi in (("kb", -14, 24), ("x", -14, 24), ("w", -30, 30)):
        v = np.abs(d[n].astype(np.float32))
        if not (np.isfinite(v).all() and ((v == 0) | (v >= 2.0 ** lo) & (v <= 2.0 ** hi)).all()): b.append("a value of " + n)
    if (d["kb"].astype(np.float32) != d["kb"][:1].astype(np.float32)).any(): b.append("kb isn't the same on all ranks")
    return b
def numbers(k, e):
    return decode(pick(k, np.concatenate([e, np.full(-len(e) % 4, -1)]))).reshape(128, -1, 4)[:, :len(e)]
def anew(k, e, v):
    t = np.zeros((128, len(e) + -len(e) % 4, 4), np.float32)
    t[:, :len(e)] = v
    return put(k, e, pick(mx_ref.quantize(t.reshape(128, -1).astype(BF)), np.arange(len(e))))
def reference(kb, x, w):
    k = join(*[mx_ref.quantize(np.ascontiguousarray(kb[r])) for r in range(N)])
    q = join(*[mx_ref.quantize(np.ascontiguousarray(x[r])) for r in range(N)])
    dx = decode(q).reshape(128, N, R, T, 4)
    ch = np.zeros((N, R, T), np.float32)
    for b in range(R):
        won, e, t = np.zeros((N, C), bool), [], []
        for r in range(N):
            v = pick(q, (r * R + b) * T + np.arange(T))
            s = np.concatenate([mx_ref.matmul(pick(k, C * r + 128 * m + np.arange(128)), v) for m in range(C // 128)])
            win = np.argmax(s + np.float32(0), axis=0)
            u, i = np.unique(win, return_index=True)
            won[r, u] = True
            e.append(C * r + u)
            t.append(dx[:, r, b, i])
            ch[r, b] = win
        e = np.concatenate(e)
        k = anew(k, e, np.float32(0.75) * numbers(k, e) + np.float32(0.25) * np.concatenate(t, axis=1))
        src, low, high = np.arange(N * C).reshape(N, C), [], []
        for r in range(N):
            p = r ^ (1 << b)
            src[r] = np.where(won[p] & ~won[r], C * p + np.arange(C), src[r])
            if r < p:
                u = np.flatnonzero(won[r] & won[p])
                low.append(C * r + u)
                high.append(C * p + u)
        low, high = np.concatenate(low), np.concatenate(high)
        if len(low):
            v = np.float32(0.5) * numbers(k, low) + np.float32(0.5) * numbers(k, high)
            k = anew(k, np.concatenate([low, high]), np.concatenate([v, v], axis=1))
        k = pick(k, src.reshape(-1))
    oc, osc, y = np.zeros((N, 128, 4 * C), np.uint8), np.zeros((N, 16, C), np.uint8), np.zeros((N, 128, O * C), np.float32)
    for r in range(N):
        t = pick(k, C * r + np.arange(C))
        oc[r], osc[r] = emit(t)
        for o in range(O): y[r, :, C * o:C * o + C] = mx_ref.matmul(mx_ref.quantize(np.ascontiguousarray(cut(w[r], o))), t)
    return {"oc": oc, "osc": osc, "ch": ch, "y": y}

@@ -1,0 +1,361 @@
+import numpy as np
+from concourse.bass import DstId, RemoteDMATransfer
+from concourse.mybir import dt, AluOpType, AxisListType, ActivationFunctionType
+
+N, R, C, TK = 8, 3, 128, 32
+F8, U8, U16, BF, F32, I32 = "float8_e4m3fn_x4", "uint8", "uint16", "bfloat16", "float32", "int32"
+
+SCRATCH = {
+    "kbs": ("sbuf", [128, 512], BF), "xs": ("sbuf", [128, 512], BF), "ws": ("sbuf", [128, 512], BF),
+    "zh": ("sbuf", [128, 516], BF), "zf": ("sbuf", [128, 516], BF),
+    "hbc": ("sbuf", [128, 512], F8), "hbs": ("sbuf", [128, 512], U8),
+    "iq": ("sbuf", [128, 48], I32), "kk": ("sbuf", [128, 48], I32), "k8": ("sbuf", [128, 8], I32),
+    "q15": ("sbuf", [128, 48], I32), "q31": ("sbuf", [128, 4], I32), "lxi": ("sbuf", [128, 48], I32),
+    "lx": ("sbuf", [128, 48], U16), "c8": ("sbuf", [128, 8], F32), "ca": ("sbuf", [128, 8], F32), "cf": ("sbuf", [128, 8], F32),
+    "lo": ("sbuf", [128, 4], F32), "hi": ("sbuf", [128, 4], F32), "wt": ("sbuf", [128, 4], F32),
+    "uc": ("sbuf", [128, 256], BF), "dr": ("sbuf", [128, 256], BF), "zz": ("sbuf", [128, 128], F32),
+    "xqc": ("sbuf", [128, 128], F8), "xqs": ("sbuf", [128, 128], U8),
+    "wqc": ("sbuf", [128, 128], F8), "wqs": ("sbuf", [128, 128], U8),
+    "dtk": ("sbuf", [128, 384], BF),
+    "fc": ("sbuf", [128, 128], F8), "fs": ("sbuf", [128, 128], U8), "ys": ("sbuf", [128, 128], F32),
+    "scn": ("sbuf", [128, 768], F32), "jnk": ("sbuf", [128, 768], BF), "cnt": ("sbuf", [128, 12], F32),
+    "ps0": ("psum", [128, 512], F32), "ps1": ("psum", [128, 512], F32), "py": ("psum", [128, 512], F32), "pe": ("psum", [128, 512], F32),
+    "pd0": ("psum", [128, 512], F32), "pd1": ("psum", [128, 512], F32), "pd2": ("psum", [128, 512], F32), "pd3": ("psum", [128, 512], F32),
+}
+for _b in range(R):
+    SCRATCH.update({
+        "xrc%d" % _b: ("sbuf", [128, 256], F8), "xrs%d" % _b: ("sbuf", [128, 256], U8),
+        "kwc%d" % _b: ("sbuf", [128, 256], F8), "kws%d" % _b: ("sbuf", [128, 256], U8),
+        "wc%d" % _b: ("sbuf", [128, 288], F8), "wsc%d" % _b: ("sbuf", [128, 288], U8),
+        "d75_%d" % _b: ("sbuf", [128, 512], BF), "da_%d" % _b: ("sbuf", [128, 512], BF), "ha_%d" % _b: ("sbuf", [128, 128], BF),
+        "nt%d" % _b: ("sbuf", [128, 512], BF), "mt%d" % _b: ("sbuf", [128, 512], BF),
+        "of%d" % _b: ("sbuf", [128, 2], U16), "pl%d" % _b: ("sbuf", [128, 2], U16),
+        "la%d" % _b: ("sbuf", [128, 8], U16), "lf%d" % _b: ("sbuf", [128, 8], U16),
+        "hl%d" % _b: ("sbuf", [128, 1], U16), "hc%d" % _b: ("sbuf", [128, 32], F8), "hz%d" % _b: ("sbuf", [128, 32], U8),
+    })
+    for _s in "op":
+        SCRATCH.update({"%sv%d" % (_s, _b): ("sbuf", [128, 4], F32), "%sa%d" % (_s, _b): ("sbuf", [128, 256], BF),
+                        "%st%d" % (_s, _b): ("sbuf", [128, 256], BF), "%sm%d" % (_s, _b): ("sbuf", [128, 256], BF),
+                        "%sw%d" % (_s, _b): ("sbuf", [128, 24], F32)})
+
+SEMAPHORES = ["ms", "zr", "ldk", "ldx", "ldw", "io", "zfd", "cs", "hb", "qk", "qx", "qw", "xc", "xz", "d0", "d1", "d2", "d3",
+              "e0", "e1", "e2", "e3", "t0", "t1", "t2", "t3", "f0", "f1", "f2", "f3", "s0", "s1", "sc0", "sc1", "ac0", "ac1", "cv",
+              "ga", "qn", "vl", "vp", "pa", "pz", "ha", "am", "qm", "pf", "pg", "ym", "ye", "st", "loc", "ucd"]
+for _b in range(R):
+    SEMAPHORES += ["%s%d" % (_n, _b) for _n in ("hl", "hc", "hz", "rl", "rc", "rz")]
+
+
+def helpers(core, dst, T, topo):
+    c = [h for h in topo.cores_of(core) if T.rank_of(h) is None and topo.die(h) == topo.die(core) and topo.may_write(h, dst)]
+    return c[0], c[-1]
+
+
+def bits(engines):
+    return sum(1 << e for e in engines)
+
+
+NE = 8
+
+
+def hand_on(g, core, T, topo):
+    home = [c for c in topo.cores_of(core) if T.rank_of(c) is not None]
+    if not home:
+        return
+    r, sent = T.rank_of(home[0]), 0
+    for b in range(R):
+        dst = T.cores[r ^ (1 << b)]
+        ha, hb = helpers(home[0], dst, T, topo)
+        if core not in (ha, hb):
+            continue
+        rid, pid = topo.addr(dst, core)
+        eng = topo.engines(core, dst)[:NE]
+        g.wait_ge(T.sem["hl%d" % b], NE // 2)
+        j = 0 if core == ha else 1
+        g.remote_dma(T["pl%d" % b][:, j:j + 1], T["hl%d" % b][:, 0:1], T.sem["rl%d" % b], T.sem["loc"], pid, rid, bits(eng))
+        if core == ha:
+            g.wait_ge(T.sem["hc%d" % b], NE)
+            g.remote_dma(T["wc%d" % b][:, 128:160].bitcast(dt.uint8), T["hc%d" % b][:, 0:32].bitcast(dt.uint8),
+                         T.sem["rc%d" % b], T.sem["loc"], pid, rid, bits(eng))
+        else:
+            g.wait_ge(T.sem["hz%d" % b], NE)
+            g.remote_dma(T["wsc%d" % b][:, 128:160], T["hz%d" % b][:, 0:32],
+                         T.sem["rz%d" % b], T.sem["loc"], pid, rid, bits(eng))
+        sent += 2 * len(eng)
+    if sent:
+        g.wait_ge(T.sem["loc"], sent)
+
+
+def rank_program(g, core, T, topo):
+    rank = T.rank_of(core)
+    if rank is None:
+        hand_on(g, core, T, topo)
+        return
+    A, F = AluOpType, ActivationFunctionType
+    V, S, E, Y = g.vector, g.scalar, g.tensor, g.sync
+    cnt, seen, qn = {}, {}, {"V": V, "S": S, "E": E, "Y": Y, "g": g}
+
+    def up(ins, name, n=1):
+        ins.then_inc(T.sem[name], n)
+        cnt[name] = cnt.get(name, 0) + n
+
+    def wt(q, *names):
+        for m in names:
+            if cnt.get(m, 0) > seen.get((q, m), 0):
+                qn[q].wait_ge(T.sem[m], cnt[m])
+                seen[(q, m)] = cnt[m]
+
+    def due(name, n):
+        cnt[name] = cnt.get(name, 0) + n
+
+    def mx(out, lc, ls, rc, rs, name):
+        up(E.matmul_mx(out, lc, ls, rc, rs, True, True), name)
+
+    def hb(b):
+        return T.hbc[:, 128 * b:128 * b + 128], T.hbs[:, 128 * b:128 * b + 128]
+
+    pd = [T["pd%d" % b] for b in range(4)]
+
+    up(Y.dma_start(T.kbs[:], T.kb[:]), "ldk", 16)
+    up(S.dma_start(T.xs[:, 0:384], T.x[:]), "ldx", 16)
+    up(Y.dma_start(T.ws[:], T.w[:]), "ldw", 16)
+    up(V.memset(T.zh[:], 0.5), "ms")
+    up(g.iota(T.iq[:], [[0, 48]], 0, 1), "io")
+    up(g.iota(T.kk[:], [[32, 3], [16, 2], [0, 8]], 0, 0), "io")
+    up(g.iota(T.k8[:], [[16, 8]], 0, 0), "io")
+    wt("g", "ms")
+    up(g.affine_select(T.zf[:], T.zh[:], [[-1, 516]], A.is_equal, 0.0, 3, 4), "zfd")
+    up(g.iota(T.uc[:], [[16, 8], [0, 2], [1, 16]], 0, 0, allow_small_or_imprecise_dtypes=True), "ucd")
+    up(V.memset(T.xs[:, 384:512], 0.0), "zr")
+    up(V.memset(T.zz[:], 0.0), "zr")
+    wt("V", "io")
+    up(V.tensor_scalar(T.q15[:], T.iq[:], 15, None, A.bitwise_and), "cs")
+    up(V.tensor_scalar(T.q31[:, 0:1], T.iq[:, 0:1], 31, None, A.bitwise_and), "cs")
+    wt("V", "cs")
+    up(V.tensor_tensor(T.lxi[:], T.q15[:], T.kk[:], A.add), "cs")
+    up(V.tensor_tensor(T.c8[:], T.q15[:, 0:8], T.k8[:], A.add), "cs")
+    up(V.tensor_scalar(T.lo[:, 0:1], T.q31[:, 0:1], 16, None, A.is_lt), "cs")
+    up(V.tensor_scalar(T.hi[:, 0:1], T.q31[:, 0:1], 16, None, A.is_ge), "cs")
+    up(V.tensor_scalar(T.wt[:, 0:1], T.q31[:, 0:1], -256, None, A.add), "cs")
+    wt("V", "cs")
+    up(V.tensor_copy(T.lx[:], T.lxi[:]), "cs")
+    up(V.tensor_scalar(T.ca[:], T.c8[:], -224.0, None, A.add), "cs")
+    up(V.tensor_scalar(T.cf[:], T.c8[:], -192.0, None, A.add), "cs")
+    for b in range(R):
+        up(V.memset(T["nt%d" % b][:, 0:384], 0.0), "zr")
+        up(V.memset(T["mt%d" % b][:, 0:384], 0.0), "zr")
+    wt("V", "zfd", "ldk")
+    up(V.quantize_mx(T.kwc0[:, 128:256], T.kws0[:, 128:256], T.kbs[:]), "qk") if False else None
+    for b in range(4):
+        up(V.quantize_mx(*hb(b), T.zf[:, 3 - b:515 - b]), "hb")
+    up(V.quantize_mx(T.kwc0[:, 128:256], T.kws0[:, 128:256], T.kbs[:]), "qk")
+    wt("V", "ldx", "zr", "cs")
+    up(V.quantize_mx(T.xqc[:], T.xqs[:], T.xs[:]), "qx")
+
+    def picks_x(b):
+        wt("V", "qx", "cs")
+        wt("S", "qx", "cs")
+        for h in range(2):
+            o = T.lx[:, 16 * b + 8 * h:16 * b + 8 * h + 8]
+            k = slice(128 * h, 128 * h + 128)
+            up(V.tensor_copy(T["xrc%d" % b][:, k].bitcast(dt.uint32), T.xqc[:].bitcast(dt.uint32).indirect(o)), "xc")
+            up(S.activation(T["xrs%d" % b][:, k], T.xqs[:].indirect(o), F.Copy), "xz")
+
+    picks_x(0)
+
+    def ev_v(out, src, d, e, scale):
+        wt("V", d)
+        up(V.tensor_scalar(out, src, scale, None, A.mult), e)
+
+    def ev_s(out, src, d, e, scale):
+        wt("S", d)
+        up(S.activation(out, src, F.Copy, scale=scale), e)
+
+    def slots(o, b, src, chain):
+        v, a, t, m = (T["%s%s%d" % (o, n, b)] for n in "vatm")
+        up(V.tensor_scalar(v[:, 0:1], src[:, 0:1], T.lo[:, 0:1], None, A.mult), chain)
+        wt("V", chain)
+        up(V.tensor_scalar(v[:, 1:2], src[:, 1:2], T.hi[:, 0:1], v[:, 0:1], A.mult, A.add), chain)
+        wt("V", chain, "ucd")
+        up(V.tensor_scalar(a[:], T.uc[:], v[:, 1:2], T.wt[:, 0:1], A.is_equal, A.mult), chain)
+        wt("V", chain)
+        up(V.transpose(t[:], a[:]), chain)
+        wt("V", chain)
+        up(V.tensor_tensor_scan(m[:], T.dr[:], t[:], 0.0, A.mult, A.min), chain)
+        wt("V", chain)
+        return m[:, 31:256:32]
+
+    for b in range(R):
+        KC, KS, WC, WS = (T["%s%d" % (n, b)] for n in ("kwc", "kws", "wc", "wsc"))
+        XC, XS, D75, DA, HA = (T["%s%d" % (n, b)] for n in ("xrc", "xrs", "d75_", "da_", "ha_"))
+        NT, MT, OF, PL, LA, LF = (T["%s%d" % (n, b)] for n in ("nt", "mt", "of", "pl", "la", "lf"))
+        dst = T.cores[rank ^ (1 << b)]
+        h0, h1 = helpers(core, dst, T, topo)
+        G = (KC[:, 128:256], KS[:, 128:256])
+
+        def dG(k):
+            wt("E", "e%d" % k)
+            mx(pd[k][:, 0:128], *hb(k), *G, "d%d" % k)
+
+        def score(h):
+            wt("E", "sc%d" % h)
+            mx(T["ps%d" % h][:, 0:128], XC[:, 128 * h:128 * h + 128], XS[:, 128 * h:128 * h + 128], *G, "s%d" % h)
+
+        def d75(k):
+            return D75[:, 128 * k:128 * k + 128], pd[k][:, 0:128], "d%d" % k, "e%d" % k, 1.5
+
+        def sign(h):
+            j = 2 * b + h
+            wt("S", "sc%d" % h)
+            up(S.activation(T.jnk[:, 128 * j:128 * j + 128], T.scn[:, 128 * j:128 * j + 128], F.Sign,
+                            bias=T.scn[:, 128 * j + 127:128 * j + 128], scale=-1.0, accum_out=T.cnt[:, 4 * b + h:4 * b + h + 1]), "ac%d" % h)
+
+        def scan(h):
+            j = 2 * b + h
+            wt("V", "s%d" % h)
+            up(V.tensor_tensor_scan(T.scn[:, 128 * j:128 * j + 128], T["ps%d" % h][:, 0:128], T.zz[:], -1e29, A.max, A.add), "sc%d" % h)
+
+        if b == 0:
+            dts = [T.py, T.pe, T.ps0, T.ps1]
+            wt("E", "hb", "qk")
+            dG(0)
+            dG(1)
+            wt("E", "xc", "xz")
+            score(0)
+            score(1)
+            dG(2)
+            dG(3)
+            wt("E", "qx")
+            ev_v(*d75(0))
+            ev_s(*d75(1))
+            scan(0)
+            scan(1)
+            for k in range(4):
+                if k > 1:
+                    wt("E", "sc%d" % (k - 2))
+                mx(dts[k][:, 0:128], *hb(k), T.xqc[:], T.xqs[:], "t%d" % k)
+            sign(0)
+            sign(1)
+            evt = [(T.dtk[:, 96 * k:96 * k + 96], dts[k][:, 0:96], "t%d" % k, "f%d" % k, 0.5) for k in range(4)]
+            ev_s(*d75(2))
+            ev_s(*d75(3))
+            ev_v(*evt[0])
+            ev_s(*evt[1])
+            ev_s(*evt[3])
+        else:
+            wt("E", "pf", "pg", "xc", "xz")
+            score(0)
+            score(1)
+            for k in range(4):
+                dG(k)
+            scan(0)
+            scan(1)
+            sign(0)
+            sign(1)
+            ev_v(*d75(0))
+            for k in range(1, 4):
+                ev_s(*d75(k))
+        wt("V", "ac0", "ac1")
+        up(V.tensor_copy(OF[:, 0:2], T.cnt[:, 4 * b:4 * b + 2]), "cv")
+        wt("g", "cv")
+        tr = []
+        for j, h in enumerate((h0, h1)):
+            rid, pid = topo.addr(h, core)
+            e = topo.engines(core, h)[j * NE // 2:(j + 1) * NE // 2]
+            tr.append(RemoteDMATransfer(dst_ids=[DstId(rid=rid, pnc=pid)], dma_engine_mask=bits(e), remote_sem=T.sem["hl%d" % b],
+                                        src=OF[:, j:j + 1], dst=T["hl%d" % b][:, 0:1]))
+            due("loc", len(e))
+        g.remote_dma_fused(tr, local_sem=T.sem["loc"])
+
+        wt("V", "cv")
+        for k in range(4):
+            if b == 0 and k == 1:
+                ev_v(*evt[2])
+            wt("V", "e%d" % k, "f%d" % k)
+            up(V.tensor_tensor(NT[:, 384 + k:512:4], D75[:, 128 * k:128 * k + 128].indirect(OF[:, 0:2]),
+                               T.dtk[:, 96 * k + 32 * b:96 * k + 32 * b + 32], A.add), "ga")
+        wt("V", "ga")
+        up(V.quantize_mx(KC[:, 0:128], KS[:, 0:128], NT[:]), "qn")
+        wt("g", "qn")
+        rid, pid = topo.addr(h0, core)
+        e = topo.engines(core, h0)[:NE]
+        g.remote_dma(T["hc%d" % b][:, 0:32].bitcast(dt.uint8), KC[:, 96:128].bitcast(dt.uint8), T.sem["hc%d" % b], T.sem["loc"],
+                     pid, rid, bits(e))
+        due("loc", len(e))
+        rid, pid = topo.addr(h1, core)
+        e = topo.engines(core, h1)[:NE]
+        g.remote_dma(T["hz%d" % b][:, 0:32], KS[:, 96:128], T.sem["hz%d" % b], T.sem["loc"], pid, rid, bits(e))
+        due("loc", len(e))
+        for h in range(2):
+            wt("Y", "ac%d" % h)
+            up(Y.dma_start(T.ch[b:b + 1, 16 * h:16 * h + 16], T.cnt[0:16, 4 * b + h:4 * b + h + 1]), "st", 16)
+
+        if b == 0:
+            up(V.memset(T.dr[:], 1.0), "zr")
+            wt("V", "zr")
+            up(V.memset(T.dr[:, 0:256:32], 0.0), "zr")
+            wt("V", "zr")
+        w = T["ow%d" % b]
+        m = slots("o", b, T.cnt[:, 4 * b:4 * b + 2], "vl")
+        up(V.tensor_tensor(w[:, 0:8], m, T.ca[:], A.min), "vl")
+        up(V.tensor_scalar(w[:, 8:16], m, 0.0, 32.0, A.is_ge, A.mult), "vl")
+        wt("V", "vl")
+        up(V.tensor_scalar(LA[:], w[:, 0:8], 256.0, None, A.add), "vl")
+        wt("V", "vl", "qn")
+        wt("S", "vl", "qn")
+        up(V.tensor_copy(WC[:, 160:288].bitcast(dt.uint32), KC[:, 96:256].bitcast(dt.uint32).indirect(LA[:])), "pa")
+        up(S.activation(WS[:, 160:288], KS[:, 96:256].indirect(LA[:]), F.Copy), "pz")
+        wt("E", "pa", "pz")
+        for k in range(4):
+            wt("E", "e%d" % k)
+            mx(pd[k][:, 0:128], *hb(k), WC[:, 160:288], WS[:, 160:288], "d%d" % k)
+            ev_s(DA[:, 128 * k:128 * k + 128], pd[k][:, 0:128], "d%d" % k, "e%d" % k, 1.0)
+        if b == 0:
+            wt("V", "ldw")
+            up(V.quantize_mx(T.wqc[:], T.wqs[:], T.ws[:]), "qw")
+        if b + 1 < R:
+            picks_x(b + 1)
+
+        due("rl%d" % b, 2 * NE)
+        wt("V", "rl%d" % b)
+        for k in range(4):
+            wt("V", "e%d" % k)
+            up(V.tensor_copy(HA[:, 32 * k:32 * k + 32], DA[:, 128 * k:128 * k + 128].indirect(PL[:, 0:2])), "ha")
+        u = T["pw%d" % b]
+        m = slots("p", b, PL, "vp")
+        up(V.tensor_tensor(u[:, 0:8], m, w[:, 8:16], A.add), "vp")
+        wt("V", "vp")
+        up(V.tensor_tensor(u[:, 8:16], u[:, 0:8], T.cf[:], A.min), "vp")
+        wt("V", "vp")
+        up(V.tensor_scalar(LF[:], u[:, 8:16], 256.0, None, A.add), "vp")
+
+        due("rc%d" % b, NE)
+        due("rz%d" % b, NE)
+        wt("E", "e0", "e1", "e2", "e3", "rc%d" % b, "rz%d" % b)
+        wt("V", "ha")
+        for k in range(4):
+            mx(pd[k][:, 0:128], *hb(k), WC[:, 128:256], WS[:, 128:256], "d%d" % k)
+            wt("V", "d%d" % k)
+            up(V.tensor_tensor(MT[:, 384 + k:512:4], pd[k][:, 0:32], HA[:, 32 * k:32 * k + 32], A.add), "e%d" % k)
+        wt("V", "e0", "e1", "e2", "e3")
+        up(V.quantize_mx(WC[:, 0:128], WS[:, 0:128], MT[:]), "qm")
+        wt("V", "qm", "vp")
+        wt("S", "qm", "vp")
+        oc, os = (T["kwc%d" % (b + 1)][:, 128:256], T["kws%d" % (b + 1)][:, 128:256]) if b + 1 < R else (T.fc[:], T.fs[:])
+        up(V.tensor_copy(oc.bitcast(dt.uint32), WC[:, 96:288].bitcast(dt.uint32).indirect(LF[:])), "pf")
+        up(S.activation(os, WS[:, 96:288].indirect(LF[:]), F.Copy), "pg")
+
+    wt("E", "pf", "pg", "qw", "f0")
+    mx(T.py[:, 0:128], T.wqc[:], T.wqs[:], T.fc[:], T.fs[:], "ym")
+    wt("Y", "pf")
+    up(Y.dma_start(T.oc[:], T.fc[:].bitcast(dt.uint8)), "st", 16)
+    wt("S", "pg")
+    for k in range(4):
+        up(S.dma_start(T.osc[4 * k:4 * k + 4, :], T.fs[32 * k:32 * k + 4, :]), "st", 16)
+    wt("V", "ym")
+    up(V.tensor_copy(T.ys[:], T.py[:, 0:128]), "ye")
+    wt("Y", "ye")
+    up(Y.dma_start(T.y[:], T.ys[:]), "st", 16)
+    wt("Y", "st")
+    for m in sorted(cnt):
+        if max([seen.get((q, m), 0) for q in qn]) < cnt[m]:
+            wt("g", m)

@@ -1,8 +1,7 @@
-import numpy as np
 from concourse.bass import DstId, RemoteDMATransfer
-from concourse.mybir import dt, AluOpType, AxisListType, ActivationFunctionType
+from concourse.mybir import dt, AluOpType, ActivationFunctionType
 
-N, R, C, TK = 8, 3, 128, 32
+R = 3
 F8, U8, U16, BF, F32, I32 = "float8_e4m3fn_x4", "uint8", "uint16", "bfloat16", "float32", "int32"
 
 SCRATCH = {
@@ -31,16 +30,17 @@ for _b in range(R):
         "nt%d" % _b: ("sbuf", [128, 512], BF), "mt%d" % _b: ("sbuf", [128, 512], BF),
         "of%d" % _b: ("sbuf", [128, 2], U16), "pl%d" % _b: ("sbuf", [128, 2], U16),
         "la%d" % _b: ("sbuf", [128, 8], U16), "lf%d" % _b: ("sbuf", [128, 8], U16),
-        "hl%d" % _b: ("sbuf", [128, 1], U16), "hc%d" % _b: ("sbuf", [128, 32], F8), "hz%d" % _b: ("sbuf", [128, 32], U8),
+        "hl%d" % _b: ("sbuf", [128, 2], U16), "hc%d" % _b: ("sbuf", [128, 32], F8), "hz%d" % _b: ("sbuf", [128, 64], U8),
     })
     for _s in "op":
         SCRATCH.update({"%sv%d" % (_s, _b): ("sbuf", [128, 4], F32), "%sa%d" % (_s, _b): ("sbuf", [128, 256], BF),
                         "%st%d" % (_s, _b): ("sbuf", [128, 256], BF), "%sm%d" % (_s, _b): ("sbuf", [128, 256], BF),
                         "%sw%d" % (_s, _b): ("sbuf", [128, 24], F32)})
 
-SEMAPHORES = ["ms", "zr", "ldk", "ldx", "ldw", "io", "zfd", "cs", "hb", "qk", "qx", "qw", "xc", "xz", "d0", "d1", "d2", "d3",
-              "e0", "e1", "e2", "e3", "t0", "t1", "t2", "t3", "f0", "f1", "f2", "f3", "s0", "s1", "sc0", "sc1", "ac0", "ac1", "cv",
-              "ga", "qn", "vl", "vp", "pa", "pz", "ha", "am", "qm", "pf", "pg", "ym", "ye", "st", "loc", "ucd"]
+SEMAPHORES = ["ms", "zr", "ldk", "ldx", "ldw", "io", "zfd", "cs", "hb0", "hb1", "hb2", "hb3", "qk", "qx", "qw", "xc", "xz",
+              "d0", "d1", "d2", "d3", "e0", "e1", "e2", "e3", "t0", "t1", "t2", "t3", "f0", "f1", "f2", "f3", "s0", "s1",
+              "sc0", "sc1", "ac0", "ac1", "cv", "ga", "qn", "vl", "vp", "pa", "pz", "ha", "qm", "pf", "pg", "ym", "ye", "st",
+              "loc", "ucd", "iq"]
 for _b in range(R):
     SEMAPHORES += ["%s%d" % (_n, _b) for _n in ("hl", "hc", "hz", "rl", "rc", "rz")]
 
@@ -54,7 +54,9 @@ def bits(engines):
     return sum(1 << e for e in engines)
 
 
-NE = 8
+def parts(engines):
+    n = len(engines)
+    return engines[:n // 4], engines[n // 4:n // 2], engines[n // 2:]
 
 
 def hand_on(g, core, T, topo):
@@ -68,19 +70,23 @@ def hand_on(g, core, T, topo):
         if core not in (ha, hb):
             continue
         rid, pid = topo.addr(dst, core)
-        eng = topo.engines(core, dst)[:NE]
-        g.wait_ge(T.sem["hl%d" % b], NE // 2)
-        j = 0 if core == ha else 1
-        g.remote_dma(T["pl%d" % b][:, j:j + 1], T["hl%d" % b][:, 0:1], T.sem["rl%d" % b], T.sem["loc"], pid, rid, bits(eng))
+        eng = topo.engines(core, dst)
+        inn = topo.engines(home[0], core)
+        pa, pb, pz = parts(inn)
+        cols = slice(0, 2) if b else (slice(0, 1) if core == ha else slice(1, 2))
+        if b == 0 or core == hb:
+            g.wait_ge(T.sem["hl%d" % b], len(inn) if b else len(inn) // 2)
+            g.remote_dma(T["pl%d" % b][:, cols], T["hl%d" % b][:, cols], T.sem["rl%d" % b], T.sem["loc"], pid, rid, bits(eng))
+            sent += len(eng)
         if core == ha:
-            g.wait_ge(T.sem["hc%d" % b], NE)
+            g.wait_ge(T.sem["hc%d" % b], len(pa) + len(pb))
             g.remote_dma(T["wc%d" % b][:, 128:160].bitcast(dt.uint8), T["hc%d" % b][:, 0:32].bitcast(dt.uint8),
                          T.sem["rc%d" % b], T.sem["loc"], pid, rid, bits(eng))
         else:
-            g.wait_ge(T.sem["hz%d" % b], NE)
-            g.remote_dma(T["wsc%d" % b][:, 128:160], T["hz%d" % b][:, 0:32],
+            g.wait_ge(T.sem["hz%d" % b], len(pz))
+            g.remote_dma(T["wsc%d" % b][:, 128:160], T["hz%d" % b][:, 32:64],
                          T.sem["rz%d" % b], T.sem["loc"], pid, rid, bits(eng))
-        sent += 2 * len(eng)
+        sent += len(eng)
     if sent:
         g.wait_ge(T.sem["loc"], sent)
 
@@ -113,43 +119,43 @@ def rank_program(g, core, T, topo):
     def hb(b):
         return T.hbc[:, 128 * b:128 * b + 128], T.hbs[:, 128 * b:128 * b + 128]
 
+    def make_hb(b):
+        wt("V", "zfd")
+        up(V.quantize_mx(*hb(b), T.zf[:, 3 - b:515 - b]), "hb%d" % b)
+
+    def send(h, e, sem, src, dst):
+        rid, pid = topo.addr(h, core)
+        due("loc", len(e))
+        return RemoteDMATransfer(dst_ids=[DstId(rid=rid, pnc=pid)], dma_engine_mask=bits(e), remote_sem=T.sem[sem], src=src, dst=dst)
+
     pd = [T["pd%d" % b] for b in range(4)]
 
-    up(Y.dma_start(T.kbs[:], T.kb[:]), "ldk", 16)
     up(S.dma_start(T.xs[:, 0:384], T.x[:]), "ldx", 16)
+    up(Y.dma_start(T.kbs[:], T.kb[:]), "ldk", 16)
     up(Y.dma_start(T.ws[:], T.w[:]), "ldw", 16)
     up(V.memset(T.zh[:], 0.5), "ms")
-    up(g.iota(T.iq[:], [[0, 48]], 0, 1), "io")
-    up(g.iota(T.kk[:], [[32, 3], [16, 2], [0, 8]], 0, 0), "io")
-    up(g.iota(T.k8[:], [[16, 8]], 0, 0), "io")
+    up(g.iota(T.iq[:], [[0, 48]], 0, 1), "iq")
+    up(g.iota(T.kk[:], [[32, 3], [16, 2], [0, 8]], 0, 0), "iq")
     wt("g", "ms")
     up(g.affine_select(T.zf[:], T.zh[:], [[-1, 516]], A.is_equal, 0.0, 3, 4), "zfd")
+    up(g.iota(T.k8[:], [[16, 8]], 0, 0), "io")
     up(g.iota(T.uc[:], [[16, 8], [0, 2], [1, 16]], 0, 0, allow_small_or_imprecise_dtypes=True), "ucd")
     up(V.memset(T.xs[:, 384:512], 0.0), "zr")
     up(V.memset(T.zz[:], 0.0), "zr")
-    wt("V", "io")
+    up(V.memset(T.nt0[:, 0:384], 0.0), "zr")
+    wt("V", "iq")
     up(V.tensor_scalar(T.q15[:], T.iq[:], 15, None, A.bitwise_and), "cs")
     up(V.tensor_scalar(T.q31[:, 0:1], T.iq[:, 0:1], 31, None, A.bitwise_and), "cs")
     wt("V", "cs")
     up(V.tensor_tensor(T.lxi[:], T.q15[:], T.kk[:], A.add), "cs")
-    up(V.tensor_tensor(T.c8[:], T.q15[:, 0:8], T.k8[:], A.add), "cs")
-    up(V.tensor_scalar(T.lo[:, 0:1], T.q31[:, 0:1], 16, None, A.is_lt), "cs")
-    up(V.tensor_scalar(T.hi[:, 0:1], T.q31[:, 0:1], 16, None, A.is_ge), "cs")
-    up(V.tensor_scalar(T.wt[:, 0:1], T.q31[:, 0:1], -256, None, A.add), "cs")
     wt("V", "cs")
     up(V.tensor_copy(T.lx[:], T.lxi[:]), "cs")
-    up(V.tensor_scalar(T.ca[:], T.c8[:], -224.0, None, A.add), "cs")
-    up(V.tensor_scalar(T.cf[:], T.c8[:], -192.0, None, A.add), "cs")
-    for b in range(R):
-        up(V.memset(T["nt%d" % b][:, 0:384], 0.0), "zr")
-        up(V.memset(T["mt%d" % b][:, 0:384], 0.0), "zr")
-    wt("V", "zfd", "ldk")
-    up(V.quantize_mx(T.kwc0[:, 128:256], T.kws0[:, 128:256], T.kbs[:]), "qk") if False else None
-    for b in range(4):
-        up(V.quantize_mx(*hb(b), T.zf[:, 3 - b:515 - b]), "hb")
-    up(V.quantize_mx(T.kwc0[:, 128:256], T.kws0[:, 128:256], T.kbs[:]), "qk")
-    wt("V", "ldx", "zr", "cs")
+    make_hb(0)
+    make_hb(1)
+    wt("V", "ldx", "zr")
     up(V.quantize_mx(T.xqc[:], T.xqs[:], T.xs[:]), "qx")
+    wt("V", "ldk")
+    up(V.quantize_mx(T.kwc0[:, 128:256], T.kws0[:, 128:256], T.kbs[:]), "qk")
 
     def picks_x(b):
         wt("V", "qx", "cs")
@@ -161,6 +167,7 @@ def rank_program(g, core, T, topo):
             up(S.activation(T["xrs%d" % b][:, k], T.xqs[:].indirect(o), F.Copy), "xz")
 
     picks_x(0)
+    make_hb(2)
 
     def ev_v(out, src, d, e, scale):
         wt("V", d)
@@ -172,17 +179,18 @@ def rank_program(g, core, T, topo):
 
     def slots(o, b, src, chain):
         v, a, t, m = (T["%s%s%d" % (o, n, b)] for n in "vatm")
-        up(V.tensor_scalar(v[:, 0:1], src[:, 0:1], T.lo[:, 0:1], None, A.mult), chain)
-        wt("V", chain)
-        up(V.tensor_scalar(v[:, 1:2], src[:, 1:2], T.hi[:, 0:1], v[:, 0:1], A.mult, A.add), chain)
-        wt("V", chain, "ucd")
-        up(V.tensor_scalar(a[:], T.uc[:], v[:, 1:2], T.wt[:, 0:1], A.is_equal, A.mult), chain)
-        wt("V", chain)
-        up(V.transpose(t[:], a[:]), chain)
-        wt("V", chain)
-        up(V.tensor_tensor_scan(m[:], T.dr[:], t[:], 0.0, A.mult, A.min), chain)
-        wt("V", chain)
-        return m[:, 31:256:32]
+
+        def step(f, *names):
+            def go():
+                wt("V", chain, *names)
+                up(f(), chain)
+            return go
+
+        return [step(lambda: V.tensor_scalar(v[:, 0:1], src[:, 0:1], T.lo[:, 0:1], None, A.mult)),
+                step(lambda: V.tensor_scalar(v[:, 1:2], src[:, 1:2], T.hi[:, 0:1], v[:, 0:1], A.mult, A.add)),
+                step(lambda: V.tensor_scalar(a[:], T.uc[:], v[:, 1:2], T.wt[:, 0:1], A.is_equal, A.mult), "ucd"),
+                step(lambda: V.transpose(t[:], a[:])),
+                step(lambda: V.tensor_tensor_scan(m[:], T.dr[:], t[:], 0.0, A.mult, A.min))], m[:, 31:256:32], step
 
     for b in range(R):
         KC, KS, WC, WS = (T["%s%d" % (n, b)] for n in ("kwc", "kws", "wc", "wsc"))
@@ -193,7 +201,7 @@ def rank_program(g, core, T, topo):
         G = (KC[:, 128:256], KS[:, 128:256])
 
         def dG(k):
-            wt("E", "e%d" % k)
+            wt("E", "e%d" % k, "hb%d" % k)
             mx(pd[k][:, 0:128], *hb(k), *G, "d%d" % k)
 
         def score(h):
@@ -216,30 +224,36 @@ def rank_program(g, core, T, topo):
 
         if b == 0:
             dts = [T.py, T.pe, T.ps0, T.ps1]
-            wt("E", "hb", "qk")
+
+            def dT(k):
+                wt("E", "qx", "hb%d" % k)
+                if k > 1:
+                    wt("E", "sc%d" % (k - 2))
+                mx(dts[k][:, 0:128], *hb(k), T.xqc[:], T.xqs[:], "t%d" % k)
+
+            evt = [(T.dtk[:, 96 * k:96 * k + 96], dts[k][:, 0:96], "t%d" % k, "f%d" % k, 0.5) for k in range(4)]
+            wt("E", "qk")
             dG(0)
             dG(1)
             wt("E", "xc", "xz")
             score(0)
             score(1)
             dG(2)
-            dG(3)
-            wt("E", "qx")
+            dT(0)
+            dT(1)
             ev_v(*d75(0))
             ev_s(*d75(1))
             scan(0)
             scan(1)
-            for k in range(4):
-                if k > 1:
-                    wt("E", "sc%d" % (k - 2))
-                mx(dts[k][:, 0:128], *hb(k), T.xqc[:], T.xqs[:], "t%d" % k)
+            make_hb(3)
+            dG(3)
+            dT(2)
+            dT(3)
             sign(0)
             sign(1)
-            evt = [(T.dtk[:, 96 * k:96 * k + 96], dts[k][:, 0:96], "t%d" % k, "f%d" % k, 0.5) for k in range(4)]
             ev_s(*d75(2))
-            ev_s(*d75(3))
-            ev_v(*evt[0])
             ev_s(*evt[1])
+            ev_s(*d75(3))
             ev_s(*evt[3])
         else:
             wt("E", "pf", "pg", "xc", "xz")
@@ -257,45 +271,55 @@ def rank_program(g, core, T, topo):
         wt("V", "ac0", "ac1")
         up(V.tensor_copy(OF[:, 0:2], T.cnt[:, 4 * b:4 * b + 2]), "cv")
         wt("g", "cv")
-        tr = []
-        for j, h in enumerate((h0, h1)):
-            rid, pid = topo.addr(h, core)
-            e = topo.engines(core, h)[j * NE // 2:(j + 1) * NE // 2]
-            tr.append(RemoteDMATransfer(dst_ids=[DstId(rid=rid, pnc=pid)], dma_engine_mask=bits(e), remote_sem=T.sem["hl%d" % b],
-                                        src=OF[:, j:j + 1], dst=T["hl%d" % b][:, 0:1]))
+        if b == 0:
+            tr = []
+            for j, h in enumerate((h0, h1)):
+                e = topo.engines(core, h)
+                n = len(e) // 2
+                tr.append(send(h, e[j * n:j * n + n], "hl%d" % b, OF[:, j:j + 1], T["hl%d" % b][:, j:j + 1]))
+            g.remote_dma_fused(tr, local_sem=T.sem["loc"])
+        else:
+            rid, pid = topo.addr(h1, core)
+            e = topo.engines(core, h1)
+            g.remote_dma(T["hl%d" % b][:, 0:2], OF[:, 0:2], T.sem["hl%d" % b], T.sem["loc"], pid, rid, bits(e))
             due("loc", len(e))
-        g.remote_dma_fused(tr, local_sem=T.sem["loc"])
 
         wt("V", "cv")
         for k in range(4):
-            if b == 0 and k == 1:
-                ev_v(*evt[2])
+            if b == 0 and k in (0, 2):
+                ev_v(*evt[k])
             wt("V", "e%d" % k, "f%d" % k)
             up(V.tensor_tensor(NT[:, 384 + k:512:4], D75[:, 128 * k:128 * k + 128].indirect(OF[:, 0:2]),
                                T.dtk[:, 96 * k + 32 * b:96 * k + 32 * b + 32], A.add), "ga")
         wt("V", "ga")
         up(V.quantize_mx(KC[:, 0:128], KS[:, 0:128], NT[:]), "qn")
         wt("g", "qn")
-        rid, pid = topo.addr(h0, core)
-        e = topo.engines(core, h0)[:NE]
-        g.remote_dma(T["hc%d" % b][:, 0:32].bitcast(dt.uint8), KC[:, 96:128].bitcast(dt.uint8), T.sem["hc%d" % b], T.sem["loc"],
-                     pid, rid, bits(e))
-        due("loc", len(e))
-        rid, pid = topo.addr(h1, core)
-        e = topo.engines(core, h1)[:NE]
-        g.remote_dma(T["hz%d" % b][:, 0:32], KS[:, 96:128], T.sem["hz%d" % b], T.sem["loc"], pid, rid, bits(e))
-        due("loc", len(e))
+        ea, eb, ez = parts(topo.engines(core, h0))
+        g.remote_dma_fused([
+            send(h0, ea, "hc%d" % b, KC[:, 96:112].bitcast(dt.uint8), T["hc%d" % b][:, 0:16].bitcast(dt.uint8)),
+            send(h0, eb, "hc%d" % b, KC[:, 112:128].bitcast(dt.uint8), T["hc%d" % b][:, 16:32].bitcast(dt.uint8)),
+            send(h1, ez, "hz%d" % b, KS[:, 64:128], T["hz%d" % b][:, 0:64])], local_sem=T.sem["loc"])
         for h in range(2):
             wt("Y", "ac%d" % h)
             up(Y.dma_start(T.ch[b:b + 1, 16 * h:16 * h + 16], T.cnt[0:16, 4 * b + h:4 * b + h + 1]), "st", 16)
 
         if b == 0:
+            wt("V", "io")
             up(V.memset(T.dr[:], 1.0), "zr")
-            wt("V", "zr")
+            up(V.tensor_tensor(T.c8[:], T.q15[:, 0:8], T.k8[:], A.add), "cs")
+            up(V.tensor_scalar(T.lo[:, 0:1], T.q31[:, 0:1], 16, None, A.is_lt), "cs")
+            up(V.tensor_scalar(T.hi[:, 0:1], T.q31[:, 0:1], 16, None, A.is_ge), "cs")
+            up(V.tensor_scalar(T.wt[:, 0:1], T.q31[:, 0:1], -256, None, A.add), "cs")
+            wt("V", "cs", "zr")
             up(V.memset(T.dr[:, 0:256:32], 0.0), "zr")
-            wt("V", "zr")
+            up(V.tensor_scalar(T.ca[:], T.c8[:], -224.0, None, A.add), "cs")
+            up(V.tensor_scalar(T.cf[:], T.c8[:], -192.0, None, A.add), "cs")
+            wt("V", "cs", "zr")
         w = T["ow%d" % b]
-        m = slots("o", b, T.cnt[:, 4 * b:4 * b + 2], "vl")
+        steps, m, _ = slots("o", b, T.cnt[:, 4 * b:4 * b + 2], "vl")
+        for go in steps:
+            go()
+        wt("V", "vl")
         up(V.tensor_tensor(w[:, 0:8], m, T.ca[:], A.min), "vl")
         up(V.tensor_scalar(w[:, 8:16], m, 0.0, 32.0, A.is_ge, A.mult), "vl")
         wt("V", "vl")
@@ -309,33 +333,39 @@ def rank_program(g, core, T, topo):
             wt("E", "e%d" % k)
             mx(pd[k][:, 0:128], *hb(k), WC[:, 160:288], WS[:, 160:288], "d%d" % k)
             ev_s(DA[:, 128 * k:128 * k + 128], pd[k][:, 0:128], "d%d" % k, "e%d" % k, 1.0)
+        up(V.memset(MT[:, 0:384], 0.0), "zr")
+        if b + 1 < R:
+            up(V.memset(T["nt%d" % (b + 1)][:, 0:384], 0.0), "zr")
+            picks_x(b + 1)
         if b == 0:
             wt("V", "ldw")
             up(V.quantize_mx(T.wqc[:], T.wqs[:], T.ws[:]), "qw")
-        if b + 1 < R:
-            picks_x(b + 1)
 
-        due("rl%d" % b, 2 * NE)
-        wt("V", "rl%d" % b)
+        no = len(topo.engines(helpers(dst, core, T, topo)[0], core))
+        due("rl%d" % b, no if b else 2 * no)
+        wt("S", "rl%d" % b, "e0", "e1", "e2", "e3")
         for k in range(4):
-            wt("V", "e%d" % k)
-            up(V.tensor_copy(HA[:, 32 * k:32 * k + 32], DA[:, 128 * k:128 * k + 128].indirect(PL[:, 0:2])), "ha")
+            up(S.activation(HA[:, 32 * k:32 * k + 32], DA[:, 128 * k:128 * k + 128].indirect(PL[:, 0:2]), F.Copy), "ha")
+        wt("V", "rl%d" % b, "zr")
         u = T["pw%d" % b]
-        m = slots("p", b, PL, "vp")
-        up(V.tensor_tensor(u[:, 0:8], m, w[:, 8:16], A.add), "vp")
-        wt("V", "vp")
-        up(V.tensor_tensor(u[:, 8:16], u[:, 0:8], T.cf[:], A.min), "vp")
-        wt("V", "vp")
-        up(V.tensor_scalar(LF[:], u[:, 8:16], 256.0, None, A.add), "vp")
+        steps, m, step = slots("p", b, PL, "vp")
+        steps += [step(lambda: V.tensor_tensor(u[:, 0:8], m, w[:, 8:16], A.add)),
+                  step(lambda: V.tensor_tensor(u[:, 8:16], u[:, 0:8], T.cf[:], A.min)),
+                  step(lambda: V.tensor_scalar(LF[:], u[:, 8:16], 256.0, None, A.add))]
+        for go in steps[:5]:
+            go()
+        steps = steps[5:]
 
-        due("rc%d" % b, NE)
-        due("rz%d" % b, NE)
+        due("rc%d" % b, no)
+        due("rz%d" % b, no)
         wt("E", "e0", "e1", "e2", "e3", "rc%d" % b, "rz%d" % b)
         wt("V", "ha")
         for k in range(4):
             mx(pd[k][:, 0:128], *hb(k), WC[:, 128:256], WS[:, 128:256], "d%d" % k)
             wt("V", "d%d" % k)
             up(V.tensor_tensor(MT[:, 384 + k:512:4], pd[k][:, 0:32], HA[:, 32 * k:32 * k + 32], A.add), "e%d" % k)
+            if k < 3:
+                steps[k]()
         wt("V", "e0", "e1", "e2", "e3")
         up(V.quantize_mx(WC[:, 0:128], WS[:, 0:128], MT[:]), "qm")
         wt("V", "qm", "vp")

@@ -18,6 +18,7 @@ SCRATCH = {
     "dtk": ("sbuf", [128, 384], BF),
     "fc": ("sbuf", [128, 128], F8), "fs": ("sbuf", [128, 128], U8), "ys": ("sbuf", [128, 128], F32),
     "scn": ("sbuf", [128, 768], F32), "jnk": ("sbuf", [128, 768], BF), "cnt": ("sbuf", [128, 12], F32),
+    "nt": ("sbuf", [128, 512], BF), "mt": ("sbuf", [128, 512], BF),
     "ps0": ("psum", [128, 512], F32), "ps1": ("psum", [128, 512], F32), "py": ("psum", [128, 512], F32), "pe": ("psum", [128, 512], F32),
     "pd0": ("psum", [128, 512], F32), "pd1": ("psum", [128, 512], F32), "pd2": ("psum", [128, 512], F32), "pd3": ("psum", [128, 512], F32),
 }
@@ -27,7 +28,6 @@ for _b in range(R):
         "kwc%d" % _b: ("sbuf", [128, 256], F8), "kws%d" % _b: ("sbuf", [128, 256], U8),
         "wc%d" % _b: ("sbuf", [128, 288], F8), "wsc%d" % _b: ("sbuf", [128, 288], U8),
         "d75_%d" % _b: ("sbuf", [128, 512], BF), "da_%d" % _b: ("sbuf", [128, 512], BF), "ha_%d" % _b: ("sbuf", [128, 128], BF),
-        "nt%d" % _b: ("sbuf", [128, 512], BF), "mt%d" % _b: ("sbuf", [128, 512], BF),
         "of%d" % _b: ("sbuf", [128, 2], U16), "pl%d" % _b: ("sbuf", [128, 2], U16),
         "la%d" % _b: ("sbuf", [128, 8], U16), "lf%d" % _b: ("sbuf", [128, 8], U16),
         "hl%d" % _b: ("sbuf", [128, 2], U16), "hc%d" % _b: ("sbuf", [128, 32], F8), "hz%d" % _b: ("sbuf", [128, 64], U8),
@@ -37,12 +37,12 @@ for _b in range(R):
                         "%st%d" % (_s, _b): ("sbuf", [128, 256], BF), "%sm%d" % (_s, _b): ("sbuf", [128, 256], BF),
                         "%sw%d" % (_s, _b): ("sbuf", [128, 24], F32)})
 
-SEMAPHORES = ["ms", "zr", "ldk", "ldx", "ldw", "io", "zfd", "cs", "hb0", "hb1", "hb2", "hb3", "qk", "qx", "qw", "xc", "xz",
+SEMAPHORES = ["ms", "zr", "ldk", "ldx", "ldw", "io", "zfd", "cs", "c8", "hb0", "hb1", "hb2", "hb3", "qk", "qx", "qw",
               "d0", "d1", "d2", "d3", "e0", "e1", "e2", "e3", "t0", "t1", "t2", "t3", "f0", "f1", "f2", "f3", "s0", "s1",
-              "sc0", "sc1", "ac0", "ac1", "cv", "ga", "qn", "vl", "vp", "pa", "pz", "ha", "qm", "pf", "pg", "ym", "ye", "st",
-              "loc", "ucd", "iq"]
+              "m0", "m1", "m2", "m3", "n0", "n1", "n2", "n3", "sc0", "sc1", "ac0", "ac1", "cv", "ov", "ga", "qn", "vl", "vp",
+              "oc", "pa", "pz", "ha", "qm", "pf", "pg", "ym", "ye", "st", "loc", "ucd", "iq"]
 for _b in range(R):
-    SEMAPHORES += ["%s%d" % (_n, _b) for _n in ("hl", "hc", "hz", "rl", "rc", "rz")]
+    SEMAPHORES += ["%s%d" % (_n, _b) for _n in ("hl", "hc", "hz", "rl", "rc", "rz", "xc", "xz")]
 
 
 def helpers(core, dst, T, topo):
@@ -129,6 +129,7 @@ def rank_program(g, core, T, topo):
         return RemoteDMATransfer(dst_ids=[DstId(rid=rid, pnc=pid)], dma_engine_mask=bits(e), remote_sem=T.sem[sem], src=src, dst=dst)
 
     pd = [T["pd%d" % b] for b in range(4)]
+    px = [T.py, T.pe, T.ps0, T.ps1]
 
     up(S.dma_start(T.xs[:, 0:384], T.x[:]), "ldx", 16)
     up(Y.dma_start(T.kbs[:], T.kb[:]), "ldk", 16)
@@ -142,14 +143,19 @@ def rank_program(g, core, T, topo):
     up(g.iota(T.uc[:], [[16, 8], [0, 2], [1, 16]], 0, 0, allow_small_or_imprecise_dtypes=True), "ucd")
     up(V.memset(T.xs[:, 384:512], 0.0), "zr")
     up(V.memset(T.zz[:], 0.0), "zr")
-    up(V.memset(T.nt0[:, 0:384], 0.0), "zr")
+    up(V.memset(T.dr[:], 1.0), "zr")
     wt("V", "iq")
     up(V.tensor_scalar(T.q15[:], T.iq[:], 15, None, A.bitwise_and), "cs")
     up(V.tensor_scalar(T.q31[:, 0:1], T.iq[:, 0:1], 31, None, A.bitwise_and), "cs")
+    up(V.memset(T.nt[:, 0:384], 0.0), "zr")
     wt("V", "cs")
     up(V.tensor_tensor(T.lxi[:], T.q15[:], T.kk[:], A.add), "cs")
-    wt("V", "cs")
+    up(V.tensor_scalar(T.lo[:, 0:1], T.q31[:, 0:1], 16, None, A.is_lt), "cs")
+    up(V.tensor_scalar(T.hi[:, 0:1], T.q31[:, 0:1], 16, None, A.is_ge), "cs")
+    up(V.tensor_scalar(T.wt[:, 0:1], T.q31[:, 0:1], -256, None, A.add), "cs")
+    wt("V", "cs", "zr")
     up(V.tensor_copy(T.lx[:], T.lxi[:]), "cs")
+    up(V.memset(T.dr[:, 0:256:32], 0.0), "zr")
     make_hb(0)
     make_hb(1)
     wt("V", "ldx", "zr")
@@ -157,16 +163,19 @@ def rank_program(g, core, T, topo):
     wt("V", "ldk")
     up(V.quantize_mx(T.kwc0[:, 128:256], T.kws0[:, 128:256], T.kbs[:]), "qk")
 
-    def picks_x(b):
+    def pick_c(b, h):
         wt("V", "qx", "cs")
-        wt("S", "qx", "cs")
-        for h in range(2):
-            o = T.lx[:, 16 * b + 8 * h:16 * b + 8 * h + 8]
-            k = slice(128 * h, 128 * h + 128)
-            up(V.tensor_copy(T["xrc%d" % b][:, k].bitcast(dt.uint32), T.xqc[:].bitcast(dt.uint32).indirect(o)), "xc")
-            up(S.activation(T["xrs%d" % b][:, k], T.xqs[:].indirect(o), F.Copy), "xz")
+        up(V.tensor_copy(T["xrc%d" % b][:, 128 * h:128 * h + 128].bitcast(dt.uint32),
+                         T.xqc[:].bitcast(dt.uint32).indirect(T.lx[:, 16 * b + 8 * h:16 * b + 8 * h + 8])), "xc%d" % b)
 
-    picks_x(0)
+    def pick_z(b, h):
+        wt("S", "qx", "cs")
+        up(S.activation(T["xrs%d" % b][:, 128 * h:128 * h + 128],
+                        T.xqs[:].indirect(T.lx[:, 16 * b + 8 * h:16 * b + 8 * h + 8]), F.Copy), "xz%d" % b)
+
+    for h in range(2):
+        pick_c(0, h)
+        pick_z(0, h)
     make_hb(2)
 
     def ev_v(out, src, d, e, scale):
@@ -177,25 +186,25 @@ def rank_program(g, core, T, topo):
         wt("S", d)
         up(S.activation(out, src, F.Copy, scale=scale), e)
 
-    def slots(o, b, src, chain):
-        v, a, t, m = (T["%s%s%d" % (o, n, b)] for n in "vatm")
-
+    def stepper(chain):
         def step(f, *names):
             def go():
                 wt("V", chain, *names)
                 up(f(), chain)
             return go
+        return step
 
-        return [step(lambda: V.tensor_scalar(v[:, 0:1], src[:, 0:1], T.lo[:, 0:1], None, A.mult)),
-                step(lambda: V.tensor_scalar(v[:, 1:2], src[:, 1:2], T.hi[:, 0:1], v[:, 0:1], A.mult, A.add)),
-                step(lambda: V.tensor_scalar(a[:], T.uc[:], v[:, 1:2], T.wt[:, 0:1], A.is_equal, A.mult), "ucd"),
+    def slots(o, b, step, *names):
+        v, a, t, m = (T["%s%s%d" % (o, n, b)] for n in "vatm")
+        return [step(lambda: V.tensor_scalar(a[:], T.uc[:], v[:, 1:2], T.wt[:, 0:1], A.is_equal, A.mult), "ucd", *names),
                 step(lambda: V.transpose(t[:], a[:])),
-                step(lambda: V.tensor_tensor_scan(m[:], T.dr[:], t[:], 0.0, A.mult, A.min))], m[:, 31:256:32], step
+                step(lambda: V.tensor_tensor_scan(m[:], T.dr[:], t[:], 0.0, A.mult, A.min))], m[:, 31:256:32]
 
     for b in range(R):
         KC, KS, WC, WS = (T["%s%d" % (n, b)] for n in ("kwc", "kws", "wc", "wsc"))
         XC, XS, D75, DA, HA = (T["%s%d" % (n, b)] for n in ("xrc", "xrs", "d75_", "da_", "ha_"))
-        NT, MT, OF, PL, LA, LF = (T["%s%d" % (n, b)] for n in ("nt", "mt", "of", "pl", "la", "lf"))
+        OF, PL, LA, LF, ov, pv = (T["%s%d" % (n, b)] for n in ("of", "pl", "la", "lf", "ov", "pv"))
+        NT, MT = T.nt, T.mt
         dst = T.cores[rank ^ (1 << b)]
         h0, h1 = helpers(core, dst, T, topo)
         G = (KC[:, 128:256], KS[:, 128:256])
@@ -205,7 +214,7 @@ def rank_program(g, core, T, topo):
             mx(pd[k][:, 0:128], *hb(k), *G, "d%d" % k)
 
         def score(h):
-            wt("E", "sc%d" % h)
+            wt("E", "sc%d" % h, "n%d" % (2 + h))
             mx(T["ps%d" % h][:, 0:128], XC[:, 128 * h:128 * h + 128], XS[:, 128 * h:128 * h + 128], *G, "s%d" % h)
 
         def d75(k):
@@ -223,19 +232,17 @@ def rank_program(g, core, T, topo):
             up(V.tensor_tensor_scan(T.scn[:, 128 * j:128 * j + 128], T["ps%d" % h][:, 0:128], T.zz[:], -1e29, A.max, A.add), "sc%d" % h)
 
         if b == 0:
-            dts = [T.py, T.pe, T.ps0, T.ps1]
-
             def dT(k):
                 wt("E", "qx", "hb%d" % k)
                 if k > 1:
                     wt("E", "sc%d" % (k - 2))
-                mx(dts[k][:, 0:128], *hb(k), T.xqc[:], T.xqs[:], "t%d" % k)
+                mx(px[k][:, 0:128], *hb(k), T.xqc[:], T.xqs[:], "t%d" % k)
 
-            evt = [(T.dtk[:, 96 * k:96 * k + 96], dts[k][:, 0:96], "t%d" % k, "f%d" % k, 0.5) for k in range(4)]
+            evt = [(T.dtk[:, 96 * k:96 * k + 96], px[k][:, 0:96], "t%d" % k, "f%d" % k, 0.5) for k in range(4)]
             wt("E", "qk")
             dG(0)
             dG(1)
-            wt("E", "xc", "xz")
+            wt("E", "xc0", "xz0")
             score(0)
             score(1)
             dG(2)
@@ -256,11 +263,18 @@ def rank_program(g, core, T, topo):
             ev_s(*d75(3))
             ev_s(*evt[3])
         else:
-            wt("E", "pf", "pg", "xc", "xz")
+            wt("E", "pf", "pg", "xc%d" % b, "xz%d" % b)
             score(0)
             score(1)
             for k in range(4):
                 dG(k)
+            if b == 1:
+                pick_c(2, 0)
+                pick_z(2, 0)
+                pick_z(2, 1)
+            else:
+                wt("V", "ldw")
+                up(V.quantize_mx(T.wqc[:], T.wqs[:], T.ws[:]), "qw")
             scan(0)
             scan(1)
             sign(0)
@@ -270,6 +284,10 @@ def rank_program(g, core, T, topo):
                 ev_s(*d75(k))
         wt("V", "ac0", "ac1")
         up(V.tensor_copy(OF[:, 0:2], T.cnt[:, 4 * b:4 * b + 2]), "cv")
+        wt("S", "ac0", "ac1", "cs")
+        up(S.activation(ov[:, 0:1], T.cnt[:, 4 * b:4 * b + 1], F.Copy, scale=T.lo[:, 0:1]), "ov")
+        wt("S", "ov")
+        up(S.activation(ov[:, 1:2], T.cnt[:, 4 * b + 1:4 * b + 2], F.Identity, bias=ov[:, 0:1], scale=T.hi[:, 0:1]), "ov")
         wt("g", "cv")
         if b == 0:
             tr = []
@@ -303,27 +321,22 @@ def rank_program(g, core, T, topo):
             wt("Y", "ac%d" % h)
             up(Y.dma_start(T.ch[b:b + 1, 16 * h:16 * h + 16], T.cnt[0:16, 4 * b + h:4 * b + h + 1]), "st", 16)
 
+        w = T["ow%d" % b]
+        step = stepper("vl")
+        steps, m = slots("o", b, step, "ov", "cs", "zr")
+        steps[0]()
         if b == 0:
             wt("V", "io")
-            up(V.memset(T.dr[:], 1.0), "zr")
-            up(V.tensor_tensor(T.c8[:], T.q15[:, 0:8], T.k8[:], A.add), "cs")
-            up(V.tensor_scalar(T.lo[:, 0:1], T.q31[:, 0:1], 16, None, A.is_lt), "cs")
-            up(V.tensor_scalar(T.hi[:, 0:1], T.q31[:, 0:1], 16, None, A.is_ge), "cs")
-            up(V.tensor_scalar(T.wt[:, 0:1], T.q31[:, 0:1], -256, None, A.add), "cs")
-            wt("V", "cs", "zr")
-            up(V.memset(T.dr[:, 0:256:32], 0.0), "zr")
-            up(V.tensor_scalar(T.ca[:], T.c8[:], -224.0, None, A.add), "cs")
-            up(V.tensor_scalar(T.cf[:], T.c8[:], -192.0, None, A.add), "cs")
-            wt("V", "cs", "zr")
-        w = T["ow%d" % b]
-        steps, m, _ = slots("o", b, T.cnt[:, 4 * b:4 * b + 2], "vl")
-        for go in steps:
-            go()
-        wt("V", "vl")
-        up(V.tensor_tensor(w[:, 0:8], m, T.ca[:], A.min), "vl")
-        up(V.tensor_scalar(w[:, 8:16], m, 0.0, 32.0, A.is_ge, A.mult), "vl")
-        wt("V", "vl")
-        up(V.tensor_scalar(LA[:], w[:, 0:8], 256.0, None, A.add), "vl")
+            up(V.tensor_tensor(T.c8[:], T.q15[:, 0:8], T.k8[:], A.add), "c8")
+        steps[1]()
+        if b == 0:
+            wt("V", "c8")
+            up(V.tensor_scalar(T.ca[:], T.c8[:], -224.0, None, A.add), "c8")
+            up(V.tensor_scalar(T.cf[:], T.c8[:], -192.0, None, A.add), "c8")
+        steps[2]()
+        step(lambda: V.tensor_tensor(w[:, 0:8], m, T.ca[:], A.min), "c8")()
+        up(V.tensor_scalar(w[:, 8:16], m, 0.0, 32.0, A.is_ge, A.mult), "oc")
+        step(lambda: V.tensor_scalar(LA[:], w[:, 0:8], 256.0, None, A.add))()
         wt("V", "vl", "qn")
         wt("S", "vl", "qn")
         up(V.tensor_copy(WC[:, 160:288].bitcast(dt.uint32), KC[:, 96:256].bitcast(dt.uint32).indirect(LA[:])), "pa")
@@ -333,13 +346,11 @@ def rank_program(g, core, T, topo):
             wt("E", "e%d" % k)
             mx(pd[k][:, 0:128], *hb(k), WC[:, 160:288], WS[:, 160:288], "d%d" % k)
             ev_s(DA[:, 128 * k:128 * k + 128], pd[k][:, 0:128], "d%d" % k, "e%d" % k, 1.0)
-        up(V.memset(MT[:, 0:384], 0.0), "zr")
-        if b + 1 < R:
-            up(V.memset(T["nt%d" % (b + 1)][:, 0:384], 0.0), "zr")
-            picks_x(b + 1)
         if b == 0:
-            wt("V", "ldw")
-            up(V.quantize_mx(T.wqc[:], T.wqs[:], T.ws[:]), "qw")
+            up(V.memset(MT[:, 0:384], 0.0), "zr")
+            for h in range(2):
+                pick_c(1, h)
+                pick_z(1, h)
 
         no = len(topo.engines(helpers(dst, core, T, topo)[0], core))
         due("rl%d" % b, no if b else 2 * no)
@@ -348,25 +359,29 @@ def rank_program(g, core, T, topo):
             up(S.activation(HA[:, 32 * k:32 * k + 32], DA[:, 128 * k:128 * k + 128].indirect(PL[:, 0:2]), F.Copy), "ha")
         wt("V", "rl%d" % b, "zr")
         u = T["pw%d" % b]
-        steps, m, step = slots("p", b, PL, "vp")
-        steps += [step(lambda: V.tensor_tensor(u[:, 0:8], m, w[:, 8:16], A.add)),
-                  step(lambda: V.tensor_tensor(u[:, 8:16], u[:, 0:8], T.cf[:], A.min)),
-                  step(lambda: V.tensor_scalar(LF[:], u[:, 8:16], 256.0, None, A.add))]
-        for go in steps[:5]:
+        step = stepper("vp")
+        step(lambda: V.tensor_scalar(pv[:, 0:1], PL[:, 0:1], T.lo[:, 0:1], None, A.mult))()
+        step(lambda: V.tensor_scalar(pv[:, 1:2], PL[:, 1:2], T.hi[:, 0:1], pv[:, 0:1], A.mult, A.add))()
+        steps, m = slots("p", b, step)
+        for go in steps:
             go()
-        steps = steps[5:]
+        if b == 1:
+            pick_c(2, 1)
+        steps = [step(lambda: V.tensor_tensor(u[:, 0:8], m, w[:, 8:16], A.add), "oc"),
+                 step(lambda: V.tensor_tensor(u[:, 8:16], u[:, 0:8], T.cf[:], A.min)),
+                 step(lambda: V.tensor_scalar(LF[:], u[:, 8:16], 256.0, None, A.add))]
 
         due("rc%d" % b, no)
         due("rz%d" % b, no)
-        wt("E", "e0", "e1", "e2", "e3", "rc%d" % b, "rz%d" % b)
+        wt("E", "sc0", "sc1", "f0", "f1", "f2", "f3", "rc%d" % b, "rz%d" % b)
         wt("V", "ha")
         for k in range(4):
-            mx(pd[k][:, 0:128], *hb(k), WC[:, 128:256], WS[:, 128:256], "d%d" % k)
-            wt("V", "d%d" % k)
-            up(V.tensor_tensor(MT[:, 384 + k:512:4], pd[k][:, 0:32], HA[:, 32 * k:32 * k + 32], A.add), "e%d" % k)
+            mx(px[k][:, 0:128], *hb(k), WC[:, 128:256], WS[:, 128:256], "m%d" % k)
+            wt("V", "m%d" % k)
+            up(V.tensor_tensor(MT[:, 384 + k:512:4], px[k][:, 0:32], HA[:, 32 * k:32 * k + 32], A.add), "n%d" % k)
             if k < 3:
                 steps[k]()
-        wt("V", "e0", "e1", "e2", "e3")
+        wt("V", "n0", "n1", "n2", "n3")
         up(V.quantize_mx(WC[:, 0:128], WS[:, 0:128], MT[:]), "qm")
         wt("V", "qm", "vp")
         wt("S", "qm", "vp")
@@ -374,7 +389,7 @@ def rank_program(g, core, T, topo):
         up(V.tensor_copy(oc.bitcast(dt.uint32), WC[:, 96:288].bitcast(dt.uint32).indirect(LF[:])), "pf")
         up(S.activation(os, WS[:, 96:288].indirect(LF[:]), F.Copy), "pg")
 
-    wt("E", "pf", "pg", "qw", "f0")
+    wt("E", "pf", "pg", "qw", "n0")
     mx(T.py[:, 0:128], T.wqc[:], T.wqs[:], T.fc[:], T.fs[:], "ym")
     wt("Y", "pf")
     up(Y.dma_start(T.oc[:], T.fc[:].bitcast(dt.uint8)), "st", 16)

@@ -6,17 +6,18 @@ F8, U8, U16, BF, F32, I32 = "float8_e4m3fn_x4", "uint8", "uint16", "bfloat16", "
 
 SCRATCH = {
     "kbs": ("sbuf", [128, 512], BF), "xs": ("sbuf", [128, 512], BF), "ws": ("sbuf", [128, 512], BF),
-    "zh": ("sbuf", [128, 516], BF), "zf": ("sbuf", [128, 516], BF),
+    "zh": ("sbuf", [128, 128], BF), "zf": ("sbuf", [128, 516], BF),
     "hbc": ("sbuf", [128, 512], F8), "hbs": ("sbuf", [128, 512], U8),
     "iq": ("sbuf", [128, 48], I32), "kk": ("sbuf", [128, 48], I32), "k8": ("sbuf", [128, 8], I32),
     "q15": ("sbuf", [128, 48], I32), "q31": ("sbuf", [128, 4], I32), "lxi": ("sbuf", [128, 48], I32),
-    "lx": ("sbuf", [128, 48], U16), "c8": ("sbuf", [128, 8], F32), "ca": ("sbuf", [128, 8], F32), "cf": ("sbuf", [128, 8], F32),
+    "lx": ("sbuf", [128, 48], U16), "c8": ("sbuf", [128, 8], F32), "cf": ("sbuf", [128, 8], F32),
     "lo": ("sbuf", [128, 4], F32), "hi": ("sbuf", [128, 4], F32), "wt": ("sbuf", [128, 4], F32),
-    "uc": ("sbuf", [128, 256], BF), "dr": ("sbuf", [128, 256], BF), "zz": ("sbuf", [128, 128], F32),
+    "uc": ("sbuf", [128, 256], BF), "dr": ("sbuf", [128, 256], BF), "du": ("sbuf", [128, 256], BF),
     "xqc": ("sbuf", [128, 128], F8), "xqs": ("sbuf", [128, 128], U8),
     "wqc": ("sbuf", [128, 128], F8), "wqs": ("sbuf", [128, 128], U8),
     "dtk": ("sbuf", [128, 384], BF),
     "fc": ("sbuf", [128, 128], F8), "fs": ("sbuf", [128, 128], U8), "ys": ("sbuf", [128, 128], F32),
+    "zc": ("sbuf", [128, 128], F8), "zs": ("sbuf", [128, 128], U8),
     "scn": ("sbuf", [128, 768], F32), "jnk": ("sbuf", [128, 768], BF), "cnt": ("sbuf", [128, 12], F32),
     "nt": ("sbuf", [128, 512], BF), "mt": ("sbuf", [128, 512], BF),
     "ps0": ("psum", [128, 512], F32), "ps1": ("psum", [128, 512], F32), "py": ("psum", [128, 512], F32), "pe": ("psum", [128, 512], F32),
@@ -27,22 +28,22 @@ for _b in range(R):
         "xrc%d" % _b: ("sbuf", [128, 256], F8), "xrs%d" % _b: ("sbuf", [128, 256], U8),
         "kwc%d" % _b: ("sbuf", [128, 256], F8), "kws%d" % _b: ("sbuf", [128, 256], U8),
         "wc%d" % _b: ("sbuf", [128, 288], F8), "wsc%d" % _b: ("sbuf", [128, 288], U8),
-        "d75_%d" % _b: ("sbuf", [128, 512], BF), "da_%d" % _b: ("sbuf", [128, 512], BF), "ha_%d" % _b: ("sbuf", [128, 128], BF),
+        "d75_%d" % _b: ("sbuf", [128, 512], BF),
         "of%d" % _b: ("sbuf", [128, 2], U16), "pl%d" % _b: ("sbuf", [128, 2], U16),
         "la%d" % _b: ("sbuf", [128, 8], U16), "lf%d" % _b: ("sbuf", [128, 8], U16),
-        "hl%d" % _b: ("sbuf", [128, 2], U16), "hc%d" % _b: ("sbuf", [128, 32], F8), "hz%d" % _b: ("sbuf", [128, 64], U8),
+        "hl%d" % _b: ("sbuf", [128, 2], U16), "hc%d" % _b: ("sbuf", [128, 32], F8), "hz%d" % _b: ("sbuf", [128, 128], U8),
     })
     for _s in "op":
         SCRATCH.update({"%sv%d" % (_s, _b): ("sbuf", [128, 4], F32), "%sa%d" % (_s, _b): ("sbuf", [128, 256], BF),
                         "%st%d" % (_s, _b): ("sbuf", [128, 256], BF), "%sm%d" % (_s, _b): ("sbuf", [128, 256], BF),
                         "%sw%d" % (_s, _b): ("sbuf", [128, 24], F32)})
 
-SEMAPHORES = ["ms", "zr", "ldk", "ldx", "ldw", "io", "zfd", "cs", "c8", "hb0", "hb1", "hb2", "hb3", "qk", "qx", "qw",
+SEMAPHORES = ["ms", "zr", "zm", "xt", "zn", "lx", "wl", "ldk", "ldx", "ldw", "io", "zfd", "cs", "c8", "hb0", "hb1", "hb2", "hb3", "qk", "qx", "qw",
               "d0", "d1", "d2", "d3", "e0", "e1", "e2", "e3", "t0", "t1", "t2", "t3", "f0", "f1", "f2", "f3", "s0", "s1",
               "m0", "m1", "m2", "m3", "n0", "n1", "n2", "n3", "sc0", "sc1", "ac0", "ac1", "cv", "ov", "ga", "qn", "vl", "vp",
-              "oc", "pa", "pz", "ha", "qm", "pf", "pg", "ym", "ye", "st", "loc", "ucd", "iq"]
+              "oc", "pa", "pz", "zq", "pc", "ps", "zd", "qm", "pf", "pg", "ym", "ye", "st", "loc", "ucd", "iq"]
 for _b in range(R):
-    SEMAPHORES += ["%s%d" % (_n, _b) for _n in ("hl", "hc", "hz", "rl", "rc", "rz", "xc", "xz")]
+    SEMAPHORES += ["%s%d" % (_n, _b) for _n in ("hl", "hc", "hz", "rl", "rc", "rz", "xca", "xcb", "xza", "xzb")]
 
 
 def helpers(core, dst, T, topo):
@@ -55,8 +56,8 @@ def bits(engines):
 
 
 def parts(engines):
-    n = len(engines)
-    return engines[:n // 4], engines[n // 4:n // 2], engines[n // 2:]
+    n = len(engines) // 2
+    return engines[:n], engines[n:]
 
 
 def hand_on(g, core, T, topo):
@@ -72,19 +73,19 @@ def hand_on(g, core, T, topo):
         rid, pid = topo.addr(dst, core)
         eng = topo.engines(core, dst)
         inn = topo.engines(home[0], core)
-        pa, pb, pz = parts(inn)
+        pc, pz = parts(inn)
         cols = slice(0, 2) if b else (slice(0, 1) if core == ha else slice(1, 2))
         if b == 0 or core == hb:
             g.wait_ge(T.sem["hl%d" % b], len(inn) if b else len(inn) // 2)
             g.remote_dma(T["pl%d" % b][:, cols], T["hl%d" % b][:, cols], T.sem["rl%d" % b], T.sem["loc"], pid, rid, bits(eng))
             sent += len(eng)
         if core == ha:
-            g.wait_ge(T.sem["hc%d" % b], len(pa) + len(pb))
+            g.wait_ge(T.sem["hc%d" % b], len(pc))
             g.remote_dma(T["wc%d" % b][:, 128:160].bitcast(dt.uint8), T["hc%d" % b][:, 0:32].bitcast(dt.uint8),
                          T.sem["rc%d" % b], T.sem["loc"], pid, rid, bits(eng))
         else:
             g.wait_ge(T.sem["hz%d" % b], len(pz))
-            g.remote_dma(T["wsc%d" % b][:, 128:160], T["hz%d" % b][:, 32:64],
+            g.remote_dma(T["wsc%d" % b][:, 128:160], T["hz%d" % b][:, 96:128],
                          T.sem["rz%d" % b], T.sem["loc"], pid, rid, bits(eng))
         sent += len(eng)
     if sent:
@@ -113,8 +114,8 @@ def rank_program(g, core, T, topo):
     def due(name, n):
         cnt[name] = cnt.get(name, 0) + n
 
-    def mx(out, lc, ls, rc, rs, name):
-        up(E.matmul_mx(out, lc, ls, rc, rs, True, True), name)
+    def mx(out, lc, ls, rc, rs, name, start=True, stop=True):
+        up(E.matmul_mx(out, lc, ls, rc, rs, start, stop), name)
 
     def hb(b):
         return T.hbc[:, 128 * b:128 * b + 128], T.hbs[:, 128 * b:128 * b + 128]
@@ -134,49 +135,46 @@ def rank_program(g, core, T, topo):
     up(S.dma_start(T.xs[:, 0:384], T.x[:]), "ldx", 16)
     up(Y.dma_start(T.kbs[:], T.kb[:]), "ldk", 16)
     up(Y.dma_start(T.ws[:], T.w[:]), "ldw", 16)
-    up(V.memset(T.zh[:], 0.5), "ms")
     up(g.iota(T.iq[:], [[0, 48]], 0, 1), "iq")
     up(g.iota(T.kk[:], [[32, 3], [16, 2], [0, 8]], 0, 0), "iq")
+    up(V.memset(T.zf[:], 0.0), "ms")
+    up(V.memset(T.zh[:], 0.5), "ms")
     wt("g", "ms")
-    up(g.affine_select(T.zf[:], T.zh[:], [[-1, 516]], A.is_equal, 0.0, 3, 4), "zfd")
-    up(g.iota(T.k8[:], [[16, 8]], 0, 0), "io")
+    up(g.affine_select(T.zf[:, 3:515:4], T.zh[:], [[-1, 128]], A.is_equal, 0.0, 0, 1), "zfd")
     up(g.iota(T.uc[:], [[16, 8], [0, 2], [1, 16]], 0, 0, allow_small_or_imprecise_dtypes=True), "ucd")
-    up(V.memset(T.xs[:, 384:512], 0.0), "zr")
-    up(V.memset(T.zz[:], 0.0), "zr")
-    up(V.memset(T.dr[:], 1.0), "zr")
+    up(g.iota(T.k8[:], [[16, 8]], 0, 0), "io")
+    up(V.memset(T.xs[:, 384:512], 0.0), "xt")
     wt("V", "iq")
     up(V.tensor_scalar(T.q15[:], T.iq[:], 15, None, A.bitwise_and), "cs")
     up(V.tensor_scalar(T.q31[:, 0:1], T.iq[:, 0:1], 31, None, A.bitwise_and), "cs")
-    up(V.memset(T.nt[:, 0:384], 0.0), "zr")
+    up(V.memset(T.nt[:, 0:128], 0.0), "zn")
     wt("V", "cs")
     up(V.tensor_tensor(T.lxi[:], T.q15[:], T.kk[:], A.add), "cs")
-    up(V.tensor_scalar(T.lo[:, 0:1], T.q31[:, 0:1], 16, None, A.is_lt), "cs")
-    up(V.tensor_scalar(T.hi[:, 0:1], T.q31[:, 0:1], 16, None, A.is_ge), "cs")
-    up(V.tensor_scalar(T.wt[:, 0:1], T.q31[:, 0:1], -256, None, A.add), "cs")
-    wt("V", "cs", "zr")
-    up(V.tensor_copy(T.lx[:], T.lxi[:]), "cs")
-    up(V.memset(T.dr[:, 0:256:32], 0.0), "zr")
     make_hb(0)
+    wt("V", "cs")
+    up(V.tensor_copy(T.lx[:], T.lxi[:]), "lx")
     make_hb(1)
-    wt("V", "ldx", "zr")
+
+    def pick_c(b, h):
+        wt("V", "qx", "lx")
+        up(V.tensor_copy(T["xrc%d" % b][:, 128 * h:128 * h + 128].bitcast(dt.uint32),
+                         T.xqc[:].bitcast(dt.uint32).indirect(T.lx[:, 16 * b + 8 * h:16 * b + 8 * h + 8])), "xc%s%d" % ("ab"[h], b))
+
+    def pick_z(b, h):
+        wt("S", "qx", "lx")
+        up(S.activation(T["xrs%d" % b][:, 128 * h:128 * h + 128],
+                        T.xqs[:].indirect(T.lx[:, 16 * b + 8 * h:16 * b + 8 * h + 8]), F.Copy), "xz%s%d" % ("ab"[h], b))
+
+    wt("V", "ldx", "xt")
     up(V.quantize_mx(T.xqc[:], T.xqs[:], T.xs[:]), "qx")
     wt("V", "ldk")
     up(V.quantize_mx(T.kwc0[:, 128:256], T.kws0[:, 128:256], T.kbs[:]), "qk")
-
-    def pick_c(b, h):
-        wt("V", "qx", "cs")
-        up(V.tensor_copy(T["xrc%d" % b][:, 128 * h:128 * h + 128].bitcast(dt.uint32),
-                         T.xqc[:].bitcast(dt.uint32).indirect(T.lx[:, 16 * b + 8 * h:16 * b + 8 * h + 8])), "xc%d" % b)
-
-    def pick_z(b, h):
-        wt("S", "qx", "cs")
-        up(S.activation(T["xrs%d" % b][:, 128 * h:128 * h + 128],
-                        T.xqs[:].indirect(T.lx[:, 16 * b + 8 * h:16 * b + 8 * h + 8]), F.Copy), "xz%d" % b)
-
-    for h in range(2):
-        pick_c(0, h)
-        pick_z(0, h)
+    pick_c(0, 0)
+    pick_c(0, 1)
+    pick_z(0, 0)
+    pick_z(0, 1)
     make_hb(2)
+    make_hb(3)
 
     def ev_v(out, src, d, e, scale):
         wt("V", d)
@@ -194,15 +192,15 @@ def rank_program(g, core, T, topo):
             return go
         return step
 
-    def slots(o, b, step, *names):
+    def slots(o, b, step, data, op, *names):
         v, a, t, m = (T["%s%s%d" % (o, n, b)] for n in "vatm")
         return [step(lambda: V.tensor_scalar(a[:], T.uc[:], v[:, 1:2], T.wt[:, 0:1], A.is_equal, A.mult), "ucd", *names),
                 step(lambda: V.transpose(t[:], a[:])),
-                step(lambda: V.tensor_tensor_scan(m[:], T.dr[:], t[:], 0.0, A.mult, A.min))], m[:, 31:256:32]
+                step(lambda: V.tensor_tensor_scan(m[:], data[:], t[:], -1000.0, op, A.min), "zr", "c8")], m[:, 31:256:32]
 
     for b in range(R):
         KC, KS, WC, WS = (T["%s%d" % (n, b)] for n in ("kwc", "kws", "wc", "wsc"))
-        XC, XS, D75, DA, HA = (T["%s%d" % (n, b)] for n in ("xrc", "xrs", "d75_", "da_", "ha_"))
+        XC, XS, D75 = (T["%s%d" % (n, b)] for n in ("xrc", "xrs", "d75_"))
         OF, PL, LA, LF, ov, pv = (T["%s%d" % (n, b)] for n in ("of", "pl", "la", "lf", "ov", "pv"))
         NT, MT = T.nt, T.mt
         dst = T.cores[rank ^ (1 << b)]
@@ -214,7 +212,7 @@ def rank_program(g, core, T, topo):
             mx(pd[k][:, 0:128], *hb(k), *G, "d%d" % k)
 
         def score(h):
-            wt("E", "sc%d" % h, "n%d" % (2 + h))
+            wt("E", "sc%d" % h, "n%d" % (2 + h), "xc%s%d" % ("ab"[h], b), "xz%s%d" % ("ab"[h], b))
             mx(T["ps%d" % h][:, 0:128], XC[:, 128 * h:128 * h + 128], XS[:, 128 * h:128 * h + 128], *G, "s%d" % h)
 
         def d75(k):
@@ -228,50 +226,52 @@ def rank_program(g, core, T, topo):
 
         def scan(h):
             j = 2 * b + h
-            wt("V", "s%d" % h)
-            up(V.tensor_tensor_scan(T.scn[:, 128 * j:128 * j + 128], T["ps%d" % h][:, 0:128], T.zz[:], -1e29, A.max, A.add), "sc%d" % h)
+            wt("V", "s%d" % h, "zn")
+            up(V.tensor_tensor_scan(T.scn[:, 128 * j:128 * j + 128], T["ps%d" % h][:, 0:128], T.nt[:, 0:128], -1e29, A.max, A.add), "sc%d" % h)
+
+        def new(k):
+            wt("V", "cv", "e%d" % k, "f%d" % k)
+            up(V.tensor_tensor(NT[:, 384 + k:512:4], D75[:, 128 * k:128 * k + 128].indirect(OF[:, 0:2]),
+                               T.dtk[:, 96 * k + 32 * b:96 * k + 32 * b + 32], A.add), "ga")
 
         if b == 0:
+            pt = [pd[2], pd[3], T.py, T.pe]
+
             def dT(k):
                 wt("E", "qx", "hb%d" % k)
-                if k > 1:
-                    wt("E", "sc%d" % (k - 2))
-                mx(px[k][:, 0:128], *hb(k), T.xqc[:], T.xqs[:], "t%d" % k)
+                mx(pt[k][:, 0:128], *hb(k), T.xqc[:], T.xqs[:], "t%d" % k)
 
-            evt = [(T.dtk[:, 96 * k:96 * k + 96], px[k][:, 0:96], "t%d" % k, "f%d" % k, 0.5) for k in range(4)]
-            wt("E", "qk")
-            dG(0)
-            dG(1)
-            wt("E", "xc0", "xz0")
-            score(0)
-            score(1)
-            dG(2)
+            evt = [(T.dtk[:, 96 * k:96 * k + 96], pt[k][:, 0:96], "t%d" % k, "f%d" % k, 0.5) for k in range(4)]
             dT(0)
             dT(1)
-            ev_v(*d75(0))
-            ev_s(*d75(1))
-            scan(0)
-            scan(1)
-            make_hb(3)
-            dG(3)
+            wt("E", "qk")
+            score(0)
+            score(1)
+            dG(0)
+            dG(1)
             dT(2)
             dT(3)
+            ev_s(*evt[0])
+            ev_s(*evt[1])
+            wt("E", "f0", "f1")
+            dG(2)
+            dG(3)
+            scan(0)
+            scan(1)
             sign(0)
             sign(1)
-            ev_s(*d75(2))
-            ev_s(*evt[1])
-            ev_s(*d75(3))
-            ev_s(*evt[3])
+            up(V.tensor_scalar(T.lo[:, 0:1], T.q31[:, 0:1], 16, None, A.is_lt), "wl")
+            up(V.tensor_scalar(T.hi[:, 0:1], T.q31[:, 0:1], 16, None, A.is_ge), "wl")
+            up(V.tensor_scalar(T.wt[:, 0:1], T.q31[:, 0:1], -256, None, A.add), "wl")
+            ev_v(*d75(0))
         else:
-            wt("E", "pf", "pg", "xc%d" % b, "xz%d" % b)
+            wt("E", "pf", "pg")
             score(0)
             score(1)
             for k in range(4):
                 dG(k)
             if b == 1:
-                pick_c(2, 0)
-                pick_z(2, 0)
-                pick_z(2, 1)
+                pick_c(2, 1)
             else:
                 wt("V", "ldw")
                 up(V.quantize_mx(T.wqc[:], T.wqs[:], T.ws[:]), "qw")
@@ -280,14 +280,17 @@ def rank_program(g, core, T, topo):
             sign(0)
             sign(1)
             ev_v(*d75(0))
-            for k in range(1, 4):
-                ev_s(*d75(k))
+            ev_v(*d75(2))
+        wt("S", "ac0", "wl")
+        up(S.activation(ov[:, 0:1], T.cnt[:, 4 * b:4 * b + 1], F.Copy, scale=T.lo[:, 0:1]), "ov")
+        ev_s(*d75(1))
+        ev_s(*d75(3))
+        wt("S", "ac1", "ov")
+        up(S.activation(ov[:, 1:2], T.cnt[:, 4 * b + 1:4 * b + 2], F.Identity, bias=ov[:, 0:1], scale=T.hi[:, 0:1]), "ov")
+        if b == 0:
+            ev_s(*evt[3])
         wt("V", "ac0", "ac1")
         up(V.tensor_copy(OF[:, 0:2], T.cnt[:, 4 * b:4 * b + 2]), "cv")
-        wt("S", "ac0", "ac1", "cs")
-        up(S.activation(ov[:, 0:1], T.cnt[:, 4 * b:4 * b + 1], F.Copy, scale=T.lo[:, 0:1]), "ov")
-        wt("S", "ov")
-        up(S.activation(ov[:, 1:2], T.cnt[:, 4 * b + 1:4 * b + 2], F.Identity, bias=ov[:, 0:1], scale=T.hi[:, 0:1]), "ov")
         wt("g", "cv")
         if b == 0:
             tr = []
@@ -302,87 +305,85 @@ def rank_program(g, core, T, topo):
             g.remote_dma(T["hl%d" % b][:, 0:2], OF[:, 0:2], T.sem["hl%d" % b], T.sem["loc"], pid, rid, bits(e))
             due("loc", len(e))
 
-        wt("V", "cv")
-        for k in range(4):
-            if b == 0 and k in (0, 2):
-                ev_v(*evt[k])
-            wt("V", "e%d" % k, "f%d" % k)
-            up(V.tensor_tensor(NT[:, 384 + k:512:4], D75[:, 128 * k:128 * k + 128].indirect(OF[:, 0:2]),
-                               T.dtk[:, 96 * k + 32 * b:96 * k + 32 * b + 32], A.add), "ga")
-        wt("V", "ga")
+        if b == 0:
+            up(V.memset(T.nt[:, 128:384], 0.0), "zn")
+            ev_v(*d75(2))
+            ev_v(*evt[2])
+        w = T["ow%d" % b]
+        step = stepper("vl")
+        steps, m = slots("o", b, step, T.du, A.max, "ov", "wl")
+        for k in (0, 2, 1, 3):
+            new(k)
+        steps[0]()
+        wt("V", "ga", "zn")
         up(V.quantize_mx(KC[:, 0:128], KS[:, 0:128], NT[:]), "qn")
         wt("g", "qn")
-        ea, eb, ez = parts(topo.engines(core, h0))
+        ec, ez = parts(topo.engines(core, h0))
         g.remote_dma_fused([
-            send(h0, ea, "hc%d" % b, KC[:, 96:112].bitcast(dt.uint8), T["hc%d" % b][:, 0:16].bitcast(dt.uint8)),
-            send(h0, eb, "hc%d" % b, KC[:, 112:128].bitcast(dt.uint8), T["hc%d" % b][:, 16:32].bitcast(dt.uint8)),
-            send(h1, ez, "hz%d" % b, KS[:, 64:128], T["hz%d" % b][:, 0:64])], local_sem=T.sem["loc"])
+            send(h0, ec, "hc%d" % b, KC[:, 96:128].bitcast(dt.uint8), T["hc%d" % b][:, 0:32].bitcast(dt.uint8)),
+            send(h1, ez, "hz%d" % b, KS[:, 0:128], T["hz%d" % b][:, 0:128])], local_sem=T.sem["loc"])
         for h in range(2):
             wt("Y", "ac%d" % h)
             up(Y.dma_start(T.ch[b:b + 1, 16 * h:16 * h + 16], T.cnt[0:16, 4 * b + h:4 * b + h + 1]), "st", 16)
 
-        w = T["ow%d" % b]
-        step = stepper("vl")
-        steps, m = slots("o", b, step, "ov", "cs", "zr")
-        steps[0]()
+        steps[1]()
         if b == 0:
             wt("V", "io")
             up(V.tensor_tensor(T.c8[:], T.q15[:, 0:8], T.k8[:], A.add), "c8")
-        steps[1]()
-        if b == 0:
-            wt("V", "c8")
-            up(V.tensor_scalar(T.ca[:], T.c8[:], -224.0, None, A.add), "c8")
-            up(V.tensor_scalar(T.cf[:], T.c8[:], -192.0, None, A.add), "c8")
+            up(V.memset(T.du[:], -1000.0), "zr")
+            wt("V", "c8", "zr")
+            up(V.tensor_scalar(T.du[:, 0:256:32], T.c8[:], -224.0, None, A.add), "c8")
+            up(V.memset(T.dr[:], 1.0), "zr")
         steps[2]()
-        step(lambda: V.tensor_tensor(w[:, 0:8], m, T.ca[:], A.min), "c8")()
-        up(V.tensor_scalar(w[:, 8:16], m, 0.0, 32.0, A.is_ge, A.mult), "oc")
-        step(lambda: V.tensor_scalar(LA[:], w[:, 0:8], 256.0, None, A.add))()
+        step(lambda: V.tensor_scalar(LA[:], m, 256.0, None, A.add))()
+        up(V.tensor_scalar(w[:, 8:16], m, -224.0, 32.0, A.is_ge, A.mult), "oc")
         wt("V", "vl", "qn")
         wt("S", "vl", "qn")
         up(V.tensor_copy(WC[:, 160:288].bitcast(dt.uint32), KC[:, 96:256].bitcast(dt.uint32).indirect(LA[:])), "pa")
         up(S.activation(WS[:, 160:288], KS[:, 96:256].indirect(LA[:]), F.Copy), "pz")
-        wt("E", "pa", "pz")
-        for k in range(4):
-            wt("E", "e%d" % k)
-            mx(pd[k][:, 0:128], *hb(k), WC[:, 160:288], WS[:, 160:288], "d%d" % k)
-            ev_s(DA[:, 128 * k:128 * k + 128], pd[k][:, 0:128], "d%d" % k, "e%d" % k, 1.0)
         if b == 0:
-            up(V.memset(MT[:, 0:384], 0.0), "zr")
-            for h in range(2):
-                pick_c(1, h)
-                pick_z(1, h)
+            up(V.memset(MT[:], 0.0), "zm")
+            pick_c(1, 0)
+            wt("V", "zm")
+            up(V.quantize_mx(T.zc[:], T.zs[:], MT[:]), "zq")
+            up(V.memset(T.dr[:, 0:256:32], 0.0), "zr")
+            up(V.tensor_scalar(T.cf[:], T.c8[:], -192.0, None, A.add), "c8")
+            pick_c(1, 1)
+            pick_c(2, 0)
+            for k in range(2):
+                for h in range(2):
+                    pick_z(1 + k, h)
 
         no = len(topo.engines(helpers(dst, core, T, topo)[0], core))
         due("rl%d" % b, no if b else 2 * no)
-        wt("S", "rl%d" % b, "e0", "e1", "e2", "e3")
+        wt("V", "rl%d" % b, "pa", "zq", "zd")
+        wt("S", "rl%d" % b, "pz", "zq", "zd")
+        up(V.tensor_copy(T.zc[:, 0:32].bitcast(dt.uint32), WC[:, 160:288].bitcast(dt.uint32).indirect(PL[:, 0:2])), "pc")
+        up(S.activation(T.zs[:, 0:32], WS[:, 160:288].indirect(PL[:, 0:2]), F.Copy), "ps")
+        wt("E", "pc", "ps", "sc0", "sc1", "f0", "f1", "f2", "f3", "n0", "n1", "n2", "n3")
         for k in range(4):
-            up(S.activation(HA[:, 32 * k:32 * k + 32], DA[:, 128 * k:128 * k + 128].indirect(PL[:, 0:2]), F.Copy), "ha")
-        wt("V", "rl%d" % b, "zr")
+            mx(px[k][:, 0:128], *hb(k), T.zc[:], T.zs[:], "zd", True, False)
         u = T["pw%d" % b]
         step = stepper("vp")
         step(lambda: V.tensor_scalar(pv[:, 0:1], PL[:, 0:1], T.lo[:, 0:1], None, A.mult))()
         step(lambda: V.tensor_scalar(pv[:, 1:2], PL[:, 1:2], T.hi[:, 0:1], pv[:, 0:1], A.mult, A.add))()
-        steps, m = slots("p", b, step)
+        steps, m = slots("p", b, step, T.dr, A.mult)
         for go in steps:
             go()
-        if b == 1:
-            pick_c(2, 1)
-        steps = [step(lambda: V.tensor_tensor(u[:, 0:8], m, w[:, 8:16], A.add), "oc"),
-                 step(lambda: V.tensor_tensor(u[:, 8:16], u[:, 0:8], T.cf[:], A.min)),
-                 step(lambda: V.tensor_scalar(LF[:], u[:, 8:16], 256.0, None, A.add))]
+        step(lambda: V.tensor_tensor(u[:, 0:8], m, w[:, 8:16], A.add), "oc")()
+        step(lambda: V.tensor_tensor(u[:, 8:16], u[:, 0:8], T.cf[:], A.min), "c8")()
 
         due("rc%d" % b, no)
         due("rz%d" % b, no)
-        wt("E", "sc0", "sc1", "f0", "f1", "f2", "f3", "rc%d" % b, "rz%d" % b)
-        wt("V", "ha")
+        wt("E", "rc%d" % b, "rz%d" % b)
+        wt("S", "zm", "qm")
         for k in range(4):
-            mx(px[k][:, 0:128], *hb(k), WC[:, 128:256], WS[:, 128:256], "m%d" % k)
-            wt("V", "m%d" % k)
-            up(V.tensor_tensor(MT[:, 384 + k:512:4], px[k][:, 0:32], HA[:, 32 * k:32 * k + 32], A.add), "n%d" % k)
-            if k < 3:
-                steps[k]()
+            mx(px[k][:, 0:128], *hb(k), WC[:, 128:256], WS[:, 128:256], "m%d" % k, False, True)
+            wt("S", "m%d" % k)
+            up(S.activation(MT[:, 384 + k:512:4], px[k][:, 0:32], F.Copy), "n%d" % k)
         wt("V", "n0", "n1", "n2", "n3")
         up(V.quantize_mx(WC[:, 0:128], WS[:, 0:128], MT[:]), "qm")
+        step(lambda: V.tensor_scalar(LF[:], u[:, 8:16], 256.0, None, A.add))()
         wt("V", "qm", "vp")
         wt("S", "qm", "vp")
         oc, os = (T["kwc%d" % (b + 1)][:, 128:256], T["kws%d" % (b + 1)][:, 128:256]) if b + 1 < R else (T.fc[:], T.fs[:])

from concourse.bass import DstId, RemoteDMATransfer
from concourse.mybir import dt, AluOpType, ActivationFunctionType

R = 3
F8, U8, U16, BF, F32, I32 = "float8_e4m3fn_x4", "uint8", "uint16", "bfloat16", "float32", "int32"

SCRATCH = {
    "kbs": ("sbuf", [128, 512], BF), "xs": ("sbuf", [128, 512], BF), "ws": ("sbuf", [128, 512], BF),
    "zh": ("sbuf", [128, 128], BF), "zf": ("sbuf", [128, 516], BF),
    "hbc": ("sbuf", [128, 512], F8), "hbs": ("sbuf", [128, 512], U8),
    "iq": ("sbuf", [128, 48], I32), "kk": ("sbuf", [128, 48], I32), "k8": ("sbuf", [128, 8], I32),
    "q15": ("sbuf", [128, 48], I32), "q31": ("sbuf", [128, 4], I32), "lxi": ("sbuf", [128, 48], I32),
    "lx": ("sbuf", [128, 48], U16), "c8": ("sbuf", [128, 8], F32), "cf": ("sbuf", [128, 8], F32),
    "lo": ("sbuf", [128, 4], F32), "hi": ("sbuf", [128, 4], F32), "wt": ("sbuf", [128, 4], F32),
    "uc": ("sbuf", [128, 256], BF), "dr": ("sbuf", [128, 256], BF), "du": ("sbuf", [128, 256], BF),
    "xqc": ("sbuf", [128, 128], F8), "xqs": ("sbuf", [128, 128], U8),
    "wqc": ("sbuf", [128, 128], F8), "wqs": ("sbuf", [128, 128], U8),
    "dtk": ("sbuf", [128, 384], BF),
    "fc": ("sbuf", [128, 128], F8), "fs": ("sbuf", [128, 128], U8), "ys": ("sbuf", [128, 128], F32),
    "zc": ("sbuf", [128, 128], F8), "zs": ("sbuf", [128, 128], U8),
    "scn": ("sbuf", [128, 768], F32), "jnk": ("sbuf", [128, 768], BF), "cnt": ("sbuf", [128, 12], F32),
    "nt": ("sbuf", [128, 512], BF), "mt": ("sbuf", [128, 512], BF),
    "ps0": ("psum", [128, 512], F32), "ps1": ("psum", [128, 512], F32), "py": ("psum", [128, 512], F32), "pe": ("psum", [128, 512], F32),
    "pd0": ("psum", [128, 512], F32), "pd1": ("psum", [128, 512], F32), "pd2": ("psum", [128, 512], F32), "pd3": ("psum", [128, 512], F32),
}
for _b in range(R):
    SCRATCH.update({
        "xrc%d" % _b: ("sbuf", [128, 256], F8), "xrs%d" % _b: ("sbuf", [128, 256], U8),
        "kwc%d" % _b: ("sbuf", [128, 256], F8), "kws%d" % _b: ("sbuf", [128, 256], U8),
        "wc%d" % _b: ("sbuf", [128, 288], F8), "wsc%d" % _b: ("sbuf", [128, 288], U8),
        "d75_%d" % _b: ("sbuf", [128, 512], BF),
        "of%d" % _b: ("sbuf", [128, 2], U16), "pl%d" % _b: ("sbuf", [128, 2], U16),
        "la%d" % _b: ("sbuf", [128, 8], U16), "lf%d" % _b: ("sbuf", [128, 8], U16),
        "hl%d" % _b: ("sbuf", [128, 2], U16), "hc%d" % _b: ("sbuf", [128, 32], F8), "hz%d" % _b: ("sbuf", [128, 128], U8),
    })
    for _s in "op":
        SCRATCH.update({"%sv%d" % (_s, _b): ("sbuf", [128, 4], F32), "%sa%d" % (_s, _b): ("sbuf", [128, 256], BF),
                        "%st%d" % (_s, _b): ("sbuf", [128, 256], BF), "%sm%d" % (_s, _b): ("sbuf", [128, 256], BF),
                        "%sw%d" % (_s, _b): ("sbuf", [128, 24], F32)})

SEMAPHORES = ["ms", "zr", "zm", "xt", "zn", "lx", "wl", "ldk", "ldx", "ldw", "io", "zfd", "cs", "c8", "hb0", "hb1", "hb2", "hb3", "qk", "qx", "qw",
              "d0", "d1", "d2", "d3", "e0", "e1", "e2", "e3", "t0", "t1", "t2", "t3", "f0", "f1", "f2", "f3", "s0", "s1",
              "m0", "m1", "m2", "m3", "n0", "n1", "n2", "n3", "sc0", "sc1", "ac0", "ac1", "cv", "ov", "ga", "qn", "vl", "vp",
              "oc", "pa", "pz", "zq", "pc", "ps", "zd", "qm", "pf", "pg", "ym", "ye", "st", "loc", "ucd", "iq"]
for _b in range(R):
    SEMAPHORES += ["%s%d" % (_n, _b) for _n in ("hl", "hc", "hz", "rl", "rc", "rz", "xca", "xcb", "xza", "xzb")]


def helpers(core, dst, T, topo):
    c = [h for h in topo.cores_of(core) if T.rank_of(h) is None and topo.die(h) == topo.die(core) and topo.may_write(h, dst)]
    return c[0], c[-1]


def bits(engines):
    return sum(1 << e for e in engines)


def parts(engines):
    n = len(engines) // 2
    return engines[:n], engines[n:]


def hand_on(g, core, T, topo):
    home = [c for c in topo.cores_of(core) if T.rank_of(c) is not None]
    if not home:
        return
    r, sent = T.rank_of(home[0]), 0
    for b in range(R):
        dst = T.cores[r ^ (1 << b)]
        ha, hb = helpers(home[0], dst, T, topo)
        if core not in (ha, hb):
            continue
        rid, pid = topo.addr(dst, core)
        eng = topo.engines(core, dst)
        inn = topo.engines(home[0], core)
        pc, pz = parts(inn)
        cols = slice(0, 2) if b else (slice(0, 1) if core == ha else slice(1, 2))
        if b == 0 or core == hb:
            g.wait_ge(T.sem["hl%d" % b], len(inn) if b else len(inn) // 2)
            g.remote_dma(T["pl%d" % b][:, cols], T["hl%d" % b][:, cols], T.sem["rl%d" % b], T.sem["loc"], pid, rid, bits(eng))
            sent += len(eng)
        if core == ha:
            g.wait_ge(T.sem["hc%d" % b], len(pc))
            g.remote_dma(T["wc%d" % b][:, 128:160].bitcast(dt.uint8), T["hc%d" % b][:, 0:32].bitcast(dt.uint8),
                         T.sem["rc%d" % b], T.sem["loc"], pid, rid, bits(eng))
        else:
            g.wait_ge(T.sem["hz%d" % b], len(pz))
            g.remote_dma(T["wsc%d" % b][:, 128:160], T["hz%d" % b][:, 96:128],
                         T.sem["rz%d" % b], T.sem["loc"], pid, rid, bits(eng))
        sent += len(eng)
    if sent:
        g.wait_ge(T.sem["loc"], sent)


def rank_program(g, core, T, topo):
    rank = T.rank_of(core)
    if rank is None:
        hand_on(g, core, T, topo)
        return
    A, F = AluOpType, ActivationFunctionType
    V, S, E, Y = g.vector, g.scalar, g.tensor, g.sync
    cnt, seen, qn = {}, {}, {"V": V, "S": S, "E": E, "Y": Y, "g": g}

    def up(ins, name, n=1):
        ins.then_inc(T.sem[name], n)
        cnt[name] = cnt.get(name, 0) + n

    def wt(q, *names):
        for m in names:
            if cnt.get(m, 0) > seen.get((q, m), 0):
                qn[q].wait_ge(T.sem[m], cnt[m])
                seen[(q, m)] = cnt[m]

    def due(name, n):
        cnt[name] = cnt.get(name, 0) + n

    def mx(out, lc, ls, rc, rs, name, start=True, stop=True):
        up(E.matmul_mx(out, lc, ls, rc, rs, start, stop), name)

    def hb(b):
        return T.hbc[:, 128 * b:128 * b + 128], T.hbs[:, 128 * b:128 * b + 128]

    def make_hb(b):
        wt("V", "zfd")
        up(V.quantize_mx(*hb(b), T.zf[:, 3 - b:515 - b]), "hb%d" % b)

    def send(h, e, sem, src, dst):
        rid, pid = topo.addr(h, core)
        due("loc", len(e))
        return RemoteDMATransfer(dst_ids=[DstId(rid=rid, pnc=pid)], dma_engine_mask=bits(e), remote_sem=T.sem[sem], src=src, dst=dst)

    pd = [T["pd%d" % b] for b in range(4)]
    px = [T.py, T.pe, T.ps0, T.ps1]

    up(S.dma_start(T.xs[:, 0:384], T.x[:]), "ldx", 16)
    up(Y.dma_start(T.kbs[:], T.kb[:]), "ldk", 16)
    up(Y.dma_start(T.ws[:], T.w[:]), "ldw", 16)
    up(g.iota(T.iq[:], [[0, 48]], 0, 1), "iq")
    up(g.iota(T.kk[:], [[32, 3], [16, 2], [0, 8]], 0, 0), "iq")
    up(V.memset(T.zf[:], 0.0), "ms")
    up(V.memset(T.zh[:], 0.5), "ms")
    wt("g", "ms")
    up(g.affine_select(T.zf[:, 3:515:4], T.zh[:], [[-1, 128]], A.is_equal, 0.0, 0, 1), "zfd")
    up(g.iota(T.uc[:], [[16, 8], [0, 2], [1, 16]], 0, 0, allow_small_or_imprecise_dtypes=True), "ucd")
    up(g.iota(T.k8[:], [[16, 8]], 0, 0), "io")
    up(V.memset(T.xs[:, 384:512], 0.0), "xt")
    wt("V", "iq")
    up(V.tensor_scalar(T.q15[:], T.iq[:], 15, None, A.bitwise_and), "cs")
    up(V.tensor_scalar(T.q31[:, 0:1], T.iq[:, 0:1], 31, None, A.bitwise_and), "cs")
    up(V.memset(T.nt[:, 0:128], 0.0), "zn")
    wt("V", "cs")
    up(V.tensor_tensor(T.lxi[:], T.q15[:], T.kk[:], A.add), "cs")
    make_hb(0)
    wt("V", "cs")
    up(V.tensor_copy(T.lx[:], T.lxi[:]), "lx")
    make_hb(1)

    def pick_c(b, h):
        wt("V", "qx", "lx")
        up(V.tensor_copy(T["xrc%d" % b][:, 128 * h:128 * h + 128].bitcast(dt.uint32),
                         T.xqc[:].bitcast(dt.uint32).indirect(T.lx[:, 16 * b + 8 * h:16 * b + 8 * h + 8])), "xc%s%d" % ("ab"[h], b))

    def pick_z(b, h):
        wt("S", "qx", "lx")
        up(S.activation(T["xrs%d" % b][:, 128 * h:128 * h + 128],
                        T.xqs[:].indirect(T.lx[:, 16 * b + 8 * h:16 * b + 8 * h + 8]), F.Copy), "xz%s%d" % ("ab"[h], b))

    wt("V", "ldx", "xt")
    up(V.quantize_mx(T.xqc[:], T.xqs[:], T.xs[:]), "qx")
    wt("V", "ldk")
    up(V.quantize_mx(T.kwc0[:, 128:256], T.kws0[:, 128:256], T.kbs[:]), "qk")
    pick_c(0, 0)
    pick_c(0, 1)
    pick_z(0, 0)
    pick_z(0, 1)
    make_hb(2)
    make_hb(3)

    def ev_v(out, src, d, e, scale):
        wt("V", d)
        up(V.tensor_scalar(out, src, scale, None, A.mult), e)

    def ev_s(out, src, d, e, scale):
        wt("S", d)
        up(S.activation(out, src, F.Copy, scale=scale), e)

    def stepper(chain):
        def step(f, *names):
            def go():
                wt("V", chain, *names)
                up(f(), chain)
            return go
        return step

    def slots(o, b, step, data, op, *names):
        v, a, t, m = (T["%s%s%d" % (o, n, b)] for n in "vatm")
        return [step(lambda: V.tensor_scalar(a[:], T.uc[:], v[:, 1:2], T.wt[:, 0:1], A.is_equal, A.mult), "ucd", *names),
                step(lambda: V.transpose(t[:], a[:])),
                step(lambda: V.tensor_tensor_scan(m[:], data[:], t[:], -1000.0, op, A.min), "zr", "c8")], m[:, 31:256:32]

    for b in range(R):
        KC, KS, WC, WS = (T["%s%d" % (n, b)] for n in ("kwc", "kws", "wc", "wsc"))
        XC, XS, D75 = (T["%s%d" % (n, b)] for n in ("xrc", "xrs", "d75_"))
        OF, PL, LA, LF, ov, pv = (T["%s%d" % (n, b)] for n in ("of", "pl", "la", "lf", "ov", "pv"))
        NT, MT = T.nt, T.mt
        dst = T.cores[rank ^ (1 << b)]
        h0, h1 = helpers(core, dst, T, topo)
        G = (KC[:, 128:256], KS[:, 128:256])

        def dG(k):
            wt("E", "e%d" % k, "hb%d" % k)
            mx(pd[k][:, 0:128], *hb(k), *G, "d%d" % k)

        def score(h):
            wt("E", "sc%d" % h, "n%d" % (2 + h), "xc%s%d" % ("ab"[h], b), "xz%s%d" % ("ab"[h], b))
            mx(T["ps%d" % h][:, 0:128], XC[:, 128 * h:128 * h + 128], XS[:, 128 * h:128 * h + 128], *G, "s%d" % h)

        def d75(k):
            return D75[:, 128 * k:128 * k + 128], pd[k][:, 0:128], "d%d" % k, "e%d" % k, 1.5

        def sign(h):
            j = 2 * b + h
            wt("S", "sc%d" % h)
            up(S.activation(T.jnk[:, 128 * j:128 * j + 128], T.scn[:, 128 * j:128 * j + 128], F.Sign,
                            bias=T.scn[:, 128 * j + 127:128 * j + 128], scale=-1.0, accum_out=T.cnt[:, 4 * b + h:4 * b + h + 1]), "ac%d" % h)

        def scan(h):
            j = 2 * b + h
            wt("V", "s%d" % h, "zn")
            up(V.tensor_tensor_scan(T.scn[:, 128 * j:128 * j + 128], T["ps%d" % h][:, 0:128], T.nt[:, 0:128], -1e29, A.max, A.add), "sc%d" % h)

        def new(k):
            wt("V", "cv", "e%d" % k, "f%d" % k)
            up(V.tensor_tensor(NT[:, 384 + k:512:4], D75[:, 128 * k:128 * k + 128].indirect(OF[:, 0:2]),
                               T.dtk[:, 96 * k + 32 * b:96 * k + 32 * b + 32], A.add), "ga")

        if b == 0:
            pt = [pd[2], pd[3], T.py, T.pe]

            def dT(k):
                wt("E", "qx", "hb%d" % k)
                mx(pt[k][:, 0:128], *hb(k), T.xqc[:], T.xqs[:], "t%d" % k)

            evt = [(T.dtk[:, 96 * k:96 * k + 96], pt[k][:, 0:96], "t%d" % k, "f%d" % k, 0.5) for k in range(4)]
            dT(0)
            dT(1)
            wt("E", "qk")
            score(0)
            score(1)
            dG(0)
            dG(1)
            dT(2)
            dT(3)
            ev_s(*evt[0])
            ev_s(*evt[1])
            wt("E", "f0", "f1")
            dG(2)
            dG(3)
            scan(0)
            scan(1)
            sign(0)
            sign(1)
            up(V.tensor_scalar(T.lo[:, 0:1], T.q31[:, 0:1], 16, None, A.is_lt), "wl")
            up(V.tensor_scalar(T.hi[:, 0:1], T.q31[:, 0:1], 16, None, A.is_ge), "wl")
            up(V.tensor_scalar(T.wt[:, 0:1], T.q31[:, 0:1], -256, None, A.add), "wl")
            ev_v(*d75(0))
        else:
            wt("E", "pf", "pg")
            score(0)
            score(1)
            for k in range(4):
                dG(k)
            if b == 1:
                pick_c(2, 1)
            else:
                wt("V", "ldw")
                up(V.quantize_mx(T.wqc[:], T.wqs[:], T.ws[:]), "qw")
            scan(0)
            scan(1)
            sign(0)
            sign(1)
            ev_v(*d75(0))
            ev_v(*d75(2))
        wt("S", "ac0", "wl")
        up(S.activation(ov[:, 0:1], T.cnt[:, 4 * b:4 * b + 1], F.Copy, scale=T.lo[:, 0:1]), "ov")
        ev_s(*d75(1))
        ev_s(*d75(3))
        wt("S", "ac1", "ov")
        up(S.activation(ov[:, 1:2], T.cnt[:, 4 * b + 1:4 * b + 2], F.Identity, bias=ov[:, 0:1], scale=T.hi[:, 0:1]), "ov")
        if b == 0:
            ev_s(*evt[3])
        wt("V", "ac0", "ac1")
        up(V.tensor_copy(OF[:, 0:2], T.cnt[:, 4 * b:4 * b + 2]), "cv")
        wt("g", "cv")
        if b == 0:
            tr = []
            for j, h in enumerate((h0, h1)):
                e = topo.engines(core, h)
                n = len(e) // 2
                tr.append(send(h, e[j * n:j * n + n], "hl%d" % b, OF[:, j:j + 1], T["hl%d" % b][:, j:j + 1]))
            g.remote_dma_fused(tr, local_sem=T.sem["loc"])
        else:
            rid, pid = topo.addr(h1, core)
            e = topo.engines(core, h1)
            g.remote_dma(T["hl%d" % b][:, 0:2], OF[:, 0:2], T.sem["hl%d" % b], T.sem["loc"], pid, rid, bits(e))
            due("loc", len(e))

        if b == 0:
            up(V.memset(T.nt[:, 128:384], 0.0), "zn")
            ev_v(*d75(2))
            ev_v(*evt[2])
        w = T["ow%d" % b]
        step = stepper("vl")
        steps, m = slots("o", b, step, T.du, A.max, "ov", "wl")
        for k in (0, 2, 1, 3):
            new(k)
        steps[0]()
        wt("V", "ga", "zn")
        up(V.quantize_mx(KC[:, 0:128], KS[:, 0:128], NT[:]), "qn")
        wt("g", "qn")
        ec, ez = parts(topo.engines(core, h0))
        g.remote_dma_fused([
            send(h0, ec, "hc%d" % b, KC[:, 96:128].bitcast(dt.uint8), T["hc%d" % b][:, 0:32].bitcast(dt.uint8)),
            send(h1, ez, "hz%d" % b, KS[:, 0:128], T["hz%d" % b][:, 0:128])], local_sem=T.sem["loc"])
        for h in range(2):
            wt("Y", "ac%d" % h)
            up(Y.dma_start(T.ch[b:b + 1, 16 * h:16 * h + 16], T.cnt[0:16, 4 * b + h:4 * b + h + 1]), "st", 16)

        steps[1]()
        if b == 0:
            wt("V", "io")
            up(V.tensor_tensor(T.c8[:], T.q15[:, 0:8], T.k8[:], A.add), "c8")
            up(V.memset(T.du[:], -1000.0), "zr")
            wt("V", "c8", "zr")
            up(V.tensor_scalar(T.du[:, 0:256:32], T.c8[:], -224.0, None, A.add), "c8")
            up(V.memset(T.dr[:], 1.0), "zr")
        steps[2]()
        step(lambda: V.tensor_scalar(LA[:], m, 256.0, None, A.add))()
        up(V.tensor_scalar(w[:, 8:16], m, -224.0, 32.0, A.is_ge, A.mult), "oc")
        wt("V", "vl", "qn")
        wt("S", "vl", "qn")
        up(V.tensor_copy(WC[:, 160:288].bitcast(dt.uint32), KC[:, 96:256].bitcast(dt.uint32).indirect(LA[:])), "pa")
        up(S.activation(WS[:, 160:288], KS[:, 96:256].indirect(LA[:]), F.Copy), "pz")
        if b == 0:
            up(V.memset(MT[:], 0.0), "zm")
            pick_c(1, 0)
            wt("V", "zm")
            up(V.quantize_mx(T.zc[:], T.zs[:], MT[:]), "zq")
            up(V.memset(T.dr[:, 0:256:32], 0.0), "zr")
            up(V.tensor_scalar(T.cf[:], T.c8[:], -192.0, None, A.add), "c8")
            pick_c(1, 1)
            pick_c(2, 0)
            for k in range(2):
                for h in range(2):
                    pick_z(1 + k, h)

        no = len(topo.engines(helpers(dst, core, T, topo)[0], core))
        due("rl%d" % b, no if b else 2 * no)
        wt("V", "rl%d" % b, "pa", "zq", "zd")
        wt("S", "rl%d" % b, "pz", "zq", "zd")
        up(V.tensor_copy(T.zc[:, 0:32].bitcast(dt.uint32), WC[:, 160:288].bitcast(dt.uint32).indirect(PL[:, 0:2])), "pc")
        up(S.activation(T.zs[:, 0:32], WS[:, 160:288].indirect(PL[:, 0:2]), F.Copy), "ps")
        wt("E", "pc", "ps", "sc0", "sc1", "f0", "f1", "f2", "f3", "n0", "n1", "n2", "n3")
        for k in range(4):
            mx(px[k][:, 0:128], *hb(k), T.zc[:], T.zs[:], "zd", True, False)
        u = T["pw%d" % b]
        step = stepper("vp")
        step(lambda: V.tensor_scalar(pv[:, 0:1], PL[:, 0:1], T.lo[:, 0:1], None, A.mult))()
        step(lambda: V.tensor_scalar(pv[:, 1:2], PL[:, 1:2], T.hi[:, 0:1], pv[:, 0:1], A.mult, A.add))()
        steps, m = slots("p", b, step, T.dr, A.mult)
        for go in steps:
            go()
        step(lambda: V.tensor_tensor(u[:, 0:8], m, w[:, 8:16], A.add), "oc")()
        step(lambda: V.tensor_tensor(u[:, 8:16], u[:, 0:8], T.cf[:], A.min), "c8")()

        due("rc%d" % b, no)
        due("rz%d" % b, no)
        wt("E", "rc%d" % b, "rz%d" % b)
        wt("S", "zm", "qm")
        for k in range(4):
            mx(px[k][:, 0:128], *hb(k), WC[:, 128:256], WS[:, 128:256], "m%d" % k, False, True)
            wt("S", "m%d" % k)
            up(S.activation(MT[:, 384 + k:512:4], px[k][:, 0:32], F.Copy), "n%d" % k)
        wt("V", "n0", "n1", "n2", "n3")
        up(V.quantize_mx(WC[:, 0:128], WS[:, 0:128], MT[:]), "qm")
        step(lambda: V.tensor_scalar(LF[:], u[:, 8:16], 256.0, None, A.add))()
        wt("V", "qm", "vp")
        wt("S", "qm", "vp")
        oc, os = (T["kwc%d" % (b + 1)][:, 128:256], T["kws%d" % (b + 1)][:, 128:256]) if b + 1 < R else (T.fc[:], T.fs[:])
        up(V.tensor_copy(oc.bitcast(dt.uint32), WC[:, 96:288].bitcast(dt.uint32).indirect(LF[:])), "pf")
        up(S.activation(os, WS[:, 96:288].indirect(LF[:]), F.Copy), "pg")

    wt("E", "pf", "pg", "qw", "n0")
    mx(T.py[:, 0:128], T.wqc[:], T.wqs[:], T.fc[:], T.fs[:], "ym")
    wt("Y", "pf")
    up(Y.dma_start(T.oc[:], T.fc[:].bitcast(dt.uint8)), "st", 16)
    wt("S", "pg")
    for k in range(4):
        up(S.dma_start(T.osc[4 * k:4 * k + 4, :], T.fs[32 * k:32 * k + 4, :]), "st", 16)
    wt("V", "ym")
    up(V.tensor_copy(T.ys[:], T.py[:, 0:128]), "ye")
    wt("Y", "ye")
    up(Y.dma_start(T.y[:], T.ys[:]), "st", 16)
    wt("Y", "st")
    for m in sorted(cnt):
        if max([seen.get((q, m), 0) for q in qn]) < cnt[m]:
            wt("g", m)
